import numpy as np
import ml_dtypes


def mxq(x, axis, fmt="e4m3"):
    dtype, down = {"e4m3": (ml_dtypes.float8_e4m3fn, 7), "e5m2": (ml_dtypes.float8_e5m2, 14)}[fmt]
    v = np.moveaxis(np.asarray(x, np.float32).astype(ml_dtypes.bfloat16).astype(np.float64), axis, -1)
    blocks = v.reshape(v.shape[:-1] + (-1, 32))
    amax = np.abs(blocks).max(-1, keepdims=True)
    byte = np.maximum(np.where(amax > 0, np.frexp(amax)[1] - 1 + 127, 0) - down, 1)
    scale = np.exp2(byte - 127.0)
    codes = (blocks / scale).astype(np.float32).astype(dtype).astype(np.float64)
    return np.moveaxis((codes * scale).reshape(v.shape), -1, axis)


WIDE = False


def mx_kscale(k):
    if not WIDE:
        return np.ones(k)
    levels = np.array([10, -10, 5, -5, 0])
    if k % 512:
        return np.exp2(np.random.permutation(np.resize(levels, k // 32))).repeat(32)
    a = np.empty((k // 512, 16))
    for p in range(k // 512):
        a[p, :8] = np.random.permutation(np.resize(levels, 8))
        for g in range(8):
            far = levels[np.abs(levels - a[p, g]) >= 10]
            a[p, g + 8] = far[np.random.randint(len(far))]
    return np.exp2(a.ravel()).repeat(32)


def f64(x):
    return np.asarray(x).astype(np.float64)


def striped(idx):
    return np.tile(idx.reshape(-1, 16).T, (8, 1)).astype(np.uint16)


def unstriped(offs):
    return offs[:16].T.reshape(-1).astype(np.int64)


def pack_weight(w):
    k, n = w.shape
    w = f64(np.asarray(w, np.float32).astype(ml_dtypes.bfloat16)).reshape(k // 32, 32, n)
    amax = np.abs(w).max(1)
    byte = np.clip(np.where(amax > 0, np.frexp(amax)[1] - 1 + 127 - 7, 1), 1, 254)
    scaled = (w * np.exp2(127.0 - byte)[:, None, :]).reshape(k, n).astype(np.float32)
    words = np.ascontiguousarray(scaled.reshape(k // 512, 128, 4, n).transpose(0, 1, 3, 2)).astype(ml_dtypes.float8_e4m3fn).view(np.uint8)
    return words, np.ascontiguousarray(byte.astype(np.uint8).reshape(k // 512, 16, n))


def unpack_weight(words, scales):
    g, p, n, _ = words.shape
    vals = np.ascontiguousarray(words).view(ml_dtypes.float8_e4m3fn).astype(np.float64) * np.repeat(np.exp2(scales.astype(np.float64) - 127.0), 8, axis=1)[..., None]
    return vals.transpose(0, 1, 3, 2).reshape(g * 512, n)


def planes(y):
    n, m = y.shape
    v = y.astype(np.float32).astype(ml_dtypes.bfloat16).astype(np.float64).reshape(n // 32, 32, m)
    top = np.abs(v).max(1)
    byte = np.clip(np.where(top > 0, np.frexp(top)[1] - 1 + 127 - 7, 1), 1, 254)
    codes = (v * np.exp2(127.0 - byte)[:, None, :]).reshape(n, m).astype(np.float32).astype(ml_dtypes.float8_e4m3fn).view(np.uint8)
    words = codes.reshape(n // 512, 128, 4, m).transpose(0, 1, 3, 2)
    return np.ascontiguousarray(words), np.ascontiguousarray(byte.astype(np.uint8).reshape(n // 512, 16, m))


K, T, S, V, N = 1024, 1024, 512, 256, 512


def setup_inputs():
    n = np.random.standard_normal
    s = mx_kscale(K)[:, None]
    near = np.random.permutation(S)
    packed_xT = pack_weight(n((K, T)) * s)
    return {
        "x_words": packed_xT[0],
        "x_scales": packed_xT[1],
        "w0": (n((K, N)) / np.sqrt(K) / s).astype(np.float32),
        "w1": (n((K, N)) / np.sqrt(K) / s).astype(np.float32),
        "w2": (n((K, N)) / np.sqrt(K) / s).astype(np.float32),
        "w3": (n((K, N)) / np.sqrt(K) / s).astype(np.float32),
        "offs": striped(np.random.permutation(T)[:S]),
        "cen": striped(np.random.permutation(S)[:V]),
        "pos1": striped(near[:V]),
        "pos2": striped(near[V:]),
        "pos3": striped(np.random.permutation(S)[:V]),
    }


def reference(x_words, x_scales, w0, w1, w2, w3, offs, cen, pos1, pos2, pos3):
    xq = unpack_weight(x_words, x_scales)[:, unstriped(offs)]
    m0 = np.tanh(mxq(f64(w1), 0, "e4m3").T @ xq)
    c0 = m0[:, unstriped(cen)]
    y = mxq(f64(w0), 0, "e4m3").T @ xq
    m1 = np.tanh(mxq(f64(w2), 0, "e4m3").T @ xq)
    c1 = m1[:, unstriped(cen)]
    m2 = np.tanh(mxq(f64(w3), 0, "e4m3").T @ xq)
    c2 = m2[:, unstriped(cen)]
    out_0 = c0 * y[:, unstriped(pos1)] + c1 * y[:, unstriped(pos2)] + c2 * y[:, unstriped(pos3)]
    return (out_0,) + planes(out_0)

@@ -1,0 +1,180 @@
+from contextlib import ExitStack
+
+import concourse.mybir as mybir
+
+K, T, S, V, N = 1024, 1024, 512, 256, 512
+FLOPS = 2 * 4 * K * S * N
+
+F32 = mybir.dt.float32
+BF16 = mybir.dt.bfloat16
+I32 = mybir.dt.int32
+U32 = mybir.dt.uint32
+U16 = mybir.dt.uint16
+U8 = mybir.dt.uint8
+FP8X4 = mybir.dt.float8_e4m3fn_x4
+MULT = mybir.AluOpType.mult
+ADD = mybir.AluOpType.add
+TANH = mybir.ActivationFunctionType.Tanh
+
+P = 128
+PACK = 4
+PASSES = K // (P * PACK)
+VECTOR_CASTS = {(0, 0, 1), (0, 1, 1), (1, 1, 1), (3, 1, 1)}
+GPSIMD_CASTS = set()
+GPSIMD_SUMS = set()
+AFTER = {"s11": "q101", "s10": "q100", "s21": "q201", "s20": "q200"}
+STEPS = """c001 c000 q001 q000 c011 c010 q011 q010 e02 e03 e00 e01 c101 c111 q101 q111 c100 q100 c110 q110 e12 e13 c201 c211 q201 q211 e10 e11 c200 q200 c210 q210 e22 e23 c301 c311 q301 q311 e20 e21 c300 q300 c310 q310 e32 e33 e30 e31 s02 s03 s00 s01 x02 x03 s12 s13 x00 x01 s10 s11 x12 x13 s22 s23 p1 x10 x11 s20 s21 p0 x22 x23 f2 x20 f3 x21 f0 f1""".split()
+SCALAR_V = 96
+
+
+def tile_picked_zmodd_tanh_po_kernel(
+    tc, x_words, x_scales, w0, w1, w2, w3, offs, cen, pos1, pos2, pos3, out_0, out_1, out_2
+):
+    nc = tc.nc
+    weights = [w0, w1, w2, w3]
+    with ExitStack() as ctx:
+        keep = ctx.enter_context(tc.tile_pool(name="keep", bufs=1))
+        psum = ctx.enter_context(tc.psum_pool(name="psum", bufs=2))
+
+        def load_list(name, dram):
+            tile = keep.tile(list(dram.shape), U16, name=name)
+            nc.sync.dma_start(tile[:], dram)
+            return tile
+
+        def load_words(g):
+            tile = keep.tile([P, T], I32, name="words%d" % g)
+            nc.sync.dma_start(tile[:], x_words[g].rearrange("p c r -> p (c r)").bitcast(I32))
+            return tile
+
+        def load_weight(w, g):
+            tile = keep.tile([P, PACK, N], F32, name="raw%d%d" % (w, g))
+            rows = weights[w][g * P * PACK : (g + 1) * P * PACK, :]
+            nc.sync.dma_start(tile[:], rows.rearrange("(p j) c -> p j c", j=PACK))
+            return tile
+
+        warm = keep.tile([P, 8], F32, name="warm")
+        warm_out = keep.tile([P, 8], F32, name="warm_out")
+        nc.vector.memset(warm[:], 0.0)
+        nc.scalar.activation(warm_out[:], warm[:], TANH)
+
+        planes = keep.tile([P, T], U8, name="planes", align_bytes=64)
+        nc.gpsimd.memset(planes[:].bitcast(I32), 0)
+
+        raw = {}
+        offs_t = load_list("offs_t", offs)
+        words = [load_words(0)]
+        for q in range(4):
+            nc.sync.dma_start(
+                planes[32 * q : 32 * q + 4 * PASSES, :].bitcast(I32),
+                x_scales[:, 4 * q : 4 * q + 4, :].bitcast(I32),
+            )
+        raw[0, 0] = load_weight(0, 0)
+        words.append(load_words(1))
+        raw[0, 1] = load_weight(0, 1)
+        pos_t = [load_list("pos%d" % d, dram) for d, dram in enumerate([pos1, pos2, pos3])]
+        cen_t = load_list("cen_t", cen)
+        for w in range(1, 4):
+            for g in range(PASSES):
+                raw[w, g] = load_weight(w, g)
+
+        picked = [keep.tile([P, S], U32, name="picked%d" % g, align_bytes=64) for g in range(PASSES)]
+        picked_scales = keep.tile([P, S], U8, name="picked_scales", align_bytes=64)
+        nc.vector.tensor_copy(picked[0][:], words[0][:].bitcast(U32).indirect(offs_t[:]))
+        nc.vector.tensor_copy(picked_scales[:], planes[:].indirect(offs_t[:]))
+        nc.vector.tensor_copy(picked[1][:], words[1][:].bitcast(U32).indirect(offs_t[:]))
+
+        grouped = {}
+        banks = {}
+        rows = {}
+        halves = {}
+        result = keep.tile([P, PACK * V], F32, name="result")
+        out_rows = out_0.rearrange("(p t) v -> p t v", t=PACK)
+
+        def half(kind, t):
+            key = "%s%d" % (kind, t // 2)
+            if key not in halves:
+                halves[key] = keep.tile([P, 2 * V], F32, name=key, tag=AFTER.get(key, key), align_bytes=64)
+            return halves[key][:, (t % 2) * V : (t % 2 + 1) * V]
+
+        def cast(w, g, h):
+            name = "q%d%d%d" % (w, g, h)
+            tile = keep.tile([P, 2, P, PACK], BF16, name=name, tag=name, align_bytes=64)
+            src = raw[w, g][:].rearrange("p j (m t) -> p m j t", t=PACK)[:, :, :, 2 * h : 2 * h + 2]
+            dst = tile[:].rearrange("p t m j -> p m j t")
+            if (w, g, h) in VECTOR_CASTS:
+                nc.vector.tensor_copy(dst, src)
+            elif (w, g, h) in GPSIMD_CASTS:
+                nc.gpsimd.tensor_scalar(dst, src, 1.0, 0.0, MULT, ADD)
+            else:
+                nc.scalar.copy(dst, src)
+            grouped[w, g, h] = tile
+
+        def multiply(w, g, h):
+            codes = keep.tile([P, 2 * P], U32, name="codes%d%d%d" % (w, g, h), align_bytes=64)
+            scales = keep.tile([P, 2 * P], U8, name="scales%d%d%d" % (w, g, h), align_bytes=64)
+            nc.vector.quantize_mx(
+                out=codes[:].bitcast(FP8X4),
+                scales=scales[:],
+                in_=grouped[w, g, h][:].rearrange("p t m j -> p (t m j)"),
+            )
+            for u in range(2):
+                t = 2 * h + u
+                if g == 0:
+                    banks[w, t] = psum.tile([P, S], F32, name="bank%d" % t)
+                cols = slice(u * P, (u + 1) * P)
+                nc.tensor.matmul_mx(
+                    out=banks[w, t][:],
+                    lhsT=codes[:, cols].bitcast(FP8X4),
+                    lhsT_scale=scales[:, cols],
+                    rhs=picked[g][:].bitcast(FP8X4),
+                    rhs_scale=picked_scales[4 * g : P, :],
+                    start=(g == 0),
+                    stop=(g == PASSES - 1),
+                )
+
+        def leave(w, t):
+            tile = keep.tile([P, S], F32, name="rows%d%d" % (w, t))
+            if w == 0:
+                nc.scalar.copy(tile[:], banks[w, t][:])
+            else:
+                nc.scalar.activation(tile[:], banks[w, t][:], TANH)
+            rows[w, t] = tile
+
+        def sample(d, t):
+            nc.vector.tensor_copy(half("s%d" % d, t), rows[0, t][:].indirect(pos_t[d][:]))
+
+        def modulate(d, t):
+            nc.vector.tensor_tensor(
+                half("x%d" % d, t), rows[d + 1, t][:].indirect(cen_t[:]), half("s%d" % d, t), MULT
+            )
+
+        def partial(h):
+            halves["p%d" % h] = keep.tile([P, 2 * V], F32, name="p%d" % h)
+            engine = nc.gpsimd if h in GPSIMD_SUMS else nc.vector
+            engine.tensor_tensor(halves["p%d" % h][:], halves["x0%d" % h][:], halves["x1%d" % h][:], ADD)
+
+        def finish(t):
+            cols = slice(t * V, (t + 1) * V)
+            nc.vector.tensor_tensor(result[:, cols], half("p", t), half("x2", t), ADD)
+            nc.sync.dma_start(out_rows[:, t, :], result[:, cols])
+
+        actions = {"c": cast, "q": multiply, "e": leave, "s": sample, "x": modulate, "p": partial, "f": finish}
+        for step in STEPS:
+            actions[step[0]](*[int(digit) for digit in step[1:]])
+
+        rounded = keep.tile([P, V * PACK], BF16, name="rounded", align_bytes=64)
+        dst = rounded[:].rearrange("p (c i t) -> p c t i", i=4, t=PACK)
+        src = result[:].rearrange("p (t c i) -> p c t i", i=4, t=PACK)
+        cut = SCALAR_V // 4
+        nc.scalar.copy(dst[:, :cut], src[:, :cut])
+        nc.vector.tensor_copy(dst[:, cut:], src[:, cut:])
+        out_codes = keep.tile([P, V], I32, name="out_codes", align_bytes=64)
+        out_scales = keep.tile([P, V], U8, name="out_scales", align_bytes=64)
+        nc.vector.quantize_mx(out=out_codes[:].bitcast(FP8X4), scales=out_scales[:], in_=rounded[:])
+        nc.sync.dma_start(out_1[0].rearrange("p c r -> p (c r)").bitcast(I32), out_codes[:])
+        for q in range(4):
+            queue = nc.scalar if q % 2 == 0 else nc.sync
+            queue.dma_start(
+                out_2[0, 4 * q : 4 * q + 4, :].bitcast(I32),
+                out_scales[32 * q : 32 * q + 4, :].bitcast(I32),
+            )

@@ -15,16 +15,16 @@ FP8X4 = mybir.dt.float8_e4m3fn_x4
 MULT = mybir.AluOpType.mult
 ADD = mybir.AluOpType.add
 TANH = mybir.ActivationFunctionType.Tanh
+IDENTITY = mybir.ActivationFunctionType.Identity
 
 P = 128
 PACK = 4
 PASSES = K // (P * PACK)
-VECTOR_CASTS = {(0, 0, 1), (0, 1, 1), (1, 1, 1), (3, 1, 1)}
-GPSIMD_CASTS = set()
-GPSIMD_SUMS = set()
-AFTER = {"s11": "q101", "s10": "q100", "s21": "q201", "s20": "q200"}
-STEPS = """c001 c000 q001 q000 c011 c010 q011 q010 e02 e03 e00 e01 c101 c111 q101 q111 c100 q100 c110 q110 e12 e13 c201 c211 q201 q211 e10 e11 c200 q200 c210 q210 e22 e23 c301 c311 q301 q311 e20 e21 c300 q300 c310 q310 e32 e33 e30 e31 s02 s03 s00 s01 x02 x03 s12 s13 x00 x01 s10 s11 x12 x13 s22 s23 p1 x10 x11 s20 s21 p0 x22 x23 f2 x20 f3 x21 f0 f1""".split()
-SCALAR_V = 96
+QUADRANTS = 4
+TAPS = 3
+MX_ALIGN = 64
+LINE = 4
+SCALAR_COLUMNS = 96
 
 
 def tile_picked_zmodd_tanh_po_kernel(
@@ -36,6 +36,34 @@ def tile_picked_zmodd_tanh_po_kernel(
         keep = ctx.enter_context(tc.tile_pool(name="keep", bufs=1))
         psum = ctx.enter_context(tc.psum_pool(name="psum", bufs=2))
 
+        rows = {
+            (w, t): keep.tile([P, S], F32, name="rows%d%d" % (w, t)) for w in range(len(weights)) for t in range(PACK)
+        }
+        sampled = {(d, t): keep.tile([P, V], F32, name="sampled%d%d" % (d, t)) for d in range(TAPS) for t in range(PACK)}
+        terms = {(d, h): keep.tile([P, 2 * V], F32, name="terms%d%d" % (d, h)) for d in range(TAPS) for h in range(2)}
+        partial = [keep.tile([P, 2 * V], F32, name="partial%d" % h) for h in range(2)]
+        result = keep.tile([P, PACK * V], F32, name="result")
+
+        def of_set(tile, t):
+            return tile[:, t * V : (t + 1) * V]
+
+        def marks(first, second):
+            bias, scale = first[:, 0:1], second[:, 0:1]
+            nc.vector.memset(bias, 0.0)
+            nc.vector.memset(scale, 1.0)
+            return bias, scale
+
+        zero = keep.tile([P, 1], F32, name="zero")
+        nc.vector.memset(zero[:], 0.0)
+        before_sum0 = of_set(result, 0)[:, 0:1]
+        nc.scalar.activation(before_sum0, zero[:], TANH)
+        before_sum2 = of_set(result, 2)[:, 0:1]
+        nc.vector.memset(before_sum2, 0.0)
+        before_tap2_pair1 = marks(sampled[2, 2], sampled[2, 3])
+        before_tap2_pair0 = marks(sampled[2, 0], sampled[2, 1])
+        before_mask0_pair1 = marks(rows[1, 2], rows[1, 3])
+        before_partials = marks(partial[1], partial[0])
+
         def load_list(name, dram):
             tile = keep.tile(list(dram.shape), U16, name=name)
             nc.sync.dma_start(tile[:], dram)
@@ -46,133 +74,176 @@ def tile_picked_zmodd_tanh_po_kernel(
             nc.sync.dma_start(tile[:], x_words[g].rearrange("p c r -> p (c r)").bitcast(I32))
             return tile
 
+        raw = {}
+
         def load_weight(w, g):
-            tile = keep.tile([P, PACK, N], F32, name="raw%d%d" % (w, g))
-            rows = weights[w][g * P * PACK : (g + 1) * P * PACK, :]
-            nc.sync.dma_start(tile[:], rows.rearrange("(p j) c -> p j c", j=PACK))
-            return tile
+            raw[w, g] = keep.tile([P, PACK, N], F32, name="raw%d%d" % (w, g))
+            k_rows = weights[w][g * P * PACK : (g + 1) * P * PACK, :]
+            nc.sync.dma_start(raw[w, g][:], k_rows.rearrange("(p j) m -> p j m", j=PACK))
 
-        warm = keep.tile([P, 8], F32, name="warm")
-        warm_out = keep.tile([P, 8], F32, name="warm_out")
-        nc.vector.memset(warm[:], 0.0)
-        nc.scalar.activation(warm_out[:], warm[:], TANH)
-
-        planes = keep.tile([P, T], U8, name="planes", align_bytes=64)
+        planes = keep.tile([P, T], U8, name="planes", align_bytes=MX_ALIGN)
         nc.gpsimd.memset(planes[:].bitcast(I32), 0)
 
-        raw = {}
-        offs_t = load_list("offs_t", offs)
         words = [load_words(0)]
-        for q in range(4):
+        offs_list = load_list("offs_list", offs)
+        for q in range(QUADRANTS):
             nc.sync.dma_start(
                 planes[32 * q : 32 * q + 4 * PASSES, :].bitcast(I32),
                 x_scales[:, 4 * q : 4 * q + 4, :].bitcast(I32),
             )
-        raw[0, 0] = load_weight(0, 0)
+        load_weight(0, 0)
         words.append(load_words(1))
-        raw[0, 1] = load_weight(0, 1)
-        pos_t = [load_list("pos%d" % d, dram) for d, dram in enumerate([pos1, pos2, pos3])]
-        cen_t = load_list("cen_t", cen)
-        for w in range(1, 4):
-            for g in range(PASSES):
-                raw[w, g] = load_weight(w, g)
+        load_weight(0, 1)
+        load_weight(1, 0)
+        pos_lists = [load_list("pos1_list", pos1)]
+        load_weight(1, 1)
+        pos_lists.append(load_list("pos2_list", pos2))
+        load_weight(2, 0)
+        pos_lists.append(load_list("pos3_list", pos3))
+        load_weight(2, 1)
+        cen_list = load_list("cen_list", cen)
+        load_weight(3, 0)
+        load_weight(3, 1)
 
-        picked = [keep.tile([P, S], U32, name="picked%d" % g, align_bytes=64) for g in range(PASSES)]
-        picked_scales = keep.tile([P, S], U8, name="picked_scales", align_bytes=64)
-        nc.vector.tensor_copy(picked[0][:], words[0][:].bitcast(U32).indirect(offs_t[:]))
-        nc.vector.tensor_copy(picked_scales[:], planes[:].indirect(offs_t[:]))
-        nc.vector.tensor_copy(picked[1][:], words[1][:].bitcast(U32).indirect(offs_t[:]))
+        picked = [keep.tile([P, S], U32, name="picked%d" % g, align_bytes=MX_ALIGN) for g in range(PASSES)]
+        picked_scales = keep.tile([P, S], U8, name="picked_scales", align_bytes=MX_ALIGN)
+        nc.vector.tensor_copy(picked[0][:], words[0][:].bitcast(U32).indirect(offs_list[:]))
+        nc.vector.tensor_copy(picked_scales[:], planes[:].indirect(offs_list[:]))
+        nc.vector.tensor_copy(picked[1][:], words[1][:].bitcast(U32).indirect(offs_list[:]))
 
-        grouped = {}
+        rounded = {}
         banks = {}
-        rows = {}
-        halves = {}
-        result = keep.tile([P, PACK * V], F32, name="result")
-        out_rows = out_0.rearrange("(p t) v -> p t v", t=PACK)
 
-        def half(kind, t):
-            key = "%s%d" % (kind, t // 2)
-            if key not in halves:
-                halves[key] = keep.tile([P, 2 * V], F32, name=key, tag=AFTER.get(key, key), align_bytes=64)
-            return halves[key][:, (t % 2) * V : (t % 2 + 1) * V]
-
-        def cast(w, g, h):
-            name = "q%d%d%d" % (w, g, h)
-            tile = keep.tile([P, 2, P, PACK], BF16, name=name, tag=name, align_bytes=64)
-            src = raw[w, g][:].rearrange("p j (m t) -> p m j t", t=PACK)[:, :, :, 2 * h : 2 * h + 2]
-            dst = tile[:].rearrange("p t m j -> p m j t")
-            if (w, g, h) in VECTOR_CASTS:
+        def round_pair(w, g, h, on_vector=False, reads=None):
+            tile = keep.tile([P, 2, P, PACK], BF16, name="rounded%d%d%d" % (w, g, h), align_bytes=MX_ALIGN)
+            src = raw[w, g][:].rearrange("p j (i t) -> p i j t", t=PACK)[:, :, :, 2 * h : 2 * h + 2]
+            dst = tile[:].rearrange("p u i j -> p i j u")
+            if on_vector:
                 nc.vector.tensor_copy(dst, src)
-            elif (w, g, h) in GPSIMD_CASTS:
-                nc.gpsimd.tensor_scalar(dst, src, 1.0, 0.0, MULT, ADD)
+            elif reads:
+                nc.scalar.activation(dst, src, IDENTITY, bias=reads[0], scale=reads[1])
             else:
                 nc.scalar.copy(dst, src)
-            grouped[w, g, h] = tile
+            rounded[w, g, h] = tile
 
-        def multiply(w, g, h):
-            codes = keep.tile([P, 2 * P], U32, name="codes%d%d%d" % (w, g, h), align_bytes=64)
-            scales = keep.tile([P, 2 * P], U8, name="scales%d%d%d" % (w, g, h), align_bytes=64)
+        def multiply_pair(w, g, h):
+            codes = keep.tile([P, 2 * P], U32, name="codes%d%d%d" % (w, g, h), align_bytes=MX_ALIGN)
+            scales = keep.tile([P, 2 * P], U8, name="scales%d%d%d" % (w, g, h), align_bytes=MX_ALIGN)
             nc.vector.quantize_mx(
                 out=codes[:].bitcast(FP8X4),
                 scales=scales[:],
-                in_=grouped[w, g, h][:].rearrange("p t m j -> p (t m j)"),
+                in_=rounded[w, g, h][:].rearrange("p u i j -> p (u i j)"),
             )
             for u in range(2):
                 t = 2 * h + u
                 if g == 0:
                     banks[w, t] = psum.tile([P, S], F32, name="bank%d" % t)
-                cols = slice(u * P, (u + 1) * P)
+                columns = slice(u * P, (u + 1) * P)
                 nc.tensor.matmul_mx(
                     out=banks[w, t][:],
-                    lhsT=codes[:, cols].bitcast(FP8X4),
-                    lhsT_scale=scales[:, cols],
+                    lhsT=codes[:, columns].bitcast(FP8X4),
+                    lhsT_scale=scales[:, columns],
                     rhs=picked[g][:].bitcast(FP8X4),
                     rhs_scale=picked_scales[4 * g : P, :],
                     start=(g == 0),
                     stop=(g == PASSES - 1),
                 )
 
-        def leave(w, t):
-            tile = keep.tile([P, S], F32, name="rows%d%d" % (w, t))
-            if w == 0:
-                nc.scalar.copy(tile[:], banks[w, t][:])
-            else:
-                nc.scalar.activation(tile[:], banks[w, t][:], TANH)
-            rows[w, t] = tile
+        def leave_y(t):
+            nc.scalar.copy(rows[0, t][:], banks[0, t][:])
+
+        def leave_mask(d, t, bias=0.0):
+            nc.scalar.activation(rows[d + 1, t][:], banks[d + 1, t][:], TANH, bias=bias)
 
         def sample(d, t):
-            nc.vector.tensor_copy(half("s%d" % d, t), rows[0, t][:].indirect(pos_t[d][:]))
+            nc.vector.tensor_copy(sampled[d, t][:], rows[0, t][:].indirect(pos_lists[d][:]))
 
         def modulate(d, t):
-            nc.vector.tensor_tensor(
-                half("x%d" % d, t), rows[d + 1, t][:].indirect(cen_t[:]), half("s%d" % d, t), MULT
-            )
+            gathered_mask = rows[d + 1, t][:].indirect(cen_list[:])
+            nc.vector.tensor_tensor(of_set(terms[d, t // 2], t % 2), gathered_mask, sampled[d, t][:], MULT)
 
-        def partial(h):
-            halves["p%d" % h] = keep.tile([P, 2 * V], F32, name="p%d" % h)
-            engine = nc.gpsimd if h in GPSIMD_SUMS else nc.vector
-            engine.tensor_tensor(halves["p%d" % h][:], halves["x0%d" % h][:], halves["x1%d" % h][:], ADD)
+        def add_first_taps(h):
+            nc.vector.tensor_tensor(partial[h][:], terms[0, h][:], terms[1, h][:], ADD)
+
+        out_rows = out_0.rearrange("(p t) v -> p t v", t=PACK)
 
         def finish(t):
-            cols = slice(t * V, (t + 1) * V)
-            nc.vector.tensor_tensor(result[:, cols], half("p", t), half("x2", t), ADD)
-            nc.sync.dma_start(out_rows[:, t, :], result[:, cols])
+            h, u = divmod(t, 2)
+            nc.vector.tensor_tensor(of_set(result, t), of_set(partial[h], u), of_set(terms[2, h], u), ADD)
+            nc.sync.dma_start(out_rows[:, t, :], of_set(result, t))
 
-        actions = {"c": cast, "q": multiply, "e": leave, "s": sample, "x": modulate, "p": partial, "f": finish}
-        for step in STEPS:
-            actions[step[0]](*[int(digit) for digit in step[1:]])
+        for g in range(PASSES):
+            round_pair(0, g, 1, on_vector=True)
+            round_pair(0, g, 0)
+            multiply_pair(0, g, 1)
+            multiply_pair(0, g, 0)
+        for t in (2, 3, 0, 1):
+            leave_y(t)
 
-        rounded = keep.tile([P, V * PACK], BF16, name="rounded", align_bytes=64)
-        dst = rounded[:].rearrange("p (c i t) -> p c t i", i=4, t=PACK)
-        src = result[:].rearrange("p (t c i) -> p c t i", i=4, t=PACK)
-        cut = SCALAR_V // 4
+        round_pair(1, 0, 1, on_vector=True)
+        sample(0, 2)
+        multiply_pair(1, 0, 1)
+        for t in (3, 0, 1):
+            sample(0, t)
+        round_pair(1, 0, 0)
+        multiply_pair(1, 0, 0)
+        round_pair(1, 1, 1)
+        sample(1, 2)
+        multiply_pair(1, 1, 1)
+        for t in (3, 0, 1):
+            sample(1, t)
+        round_pair(1, 1, 0, reads=before_tap2_pair1)
+        multiply_pair(1, 1, 0)
+        sample(2, 2)
+        sample(2, 3)
+        round_pair(2, 0, 1, reads=before_mask0_pair1)
+        multiply_pair(2, 0, 1)
+        round_pair(2, 0, 0, reads=before_tap2_pair0)
+        multiply_pair(2, 0, 0)
+        sample(2, 0)
+        sample(2, 1)
+
+        leave_mask(0, 2)
+        leave_mask(0, 3)
+        round_pair(2, 1, 1, on_vector=True)
+        modulate(0, 2)
+        multiply_pair(2, 1, 1)
+        modulate(0, 3)
+        for (w, g, h), (d, first_set) in [((2, 1, 0), (0, 0)), ((3, 0, 1), (1, 2)), ((3, 1, 1), (1, 0))]:
+            round_pair(w, g, h)
+            multiply_pair(w, g, h)
+            leave_mask(d, first_set)
+            leave_mask(d, first_set + 1)
+            modulate(d, first_set)
+            modulate(d, first_set + 1)
+        round_pair(3, 0, 0, reads=before_partials)
+        multiply_pair(3, 0, 0)
+        add_first_taps(1)
+        add_first_taps(0)
+        round_pair(3, 1, 0)
+        multiply_pair(3, 1, 0)
+
+        leave_mask(2, 2)
+        leave_mask(2, 3, bias=before_sum2)
+        leave_mask(2, 0)
+        leave_mask(2, 1, bias=before_sum0)
+        for first_set in (2, 0):
+            modulate(2, first_set)
+            modulate(2, first_set + 1)
+            finish(first_set)
+            finish(first_set + 1)
+
+        out_rounded = keep.tile([P, V * PACK], BF16, name="out_rounded", align_bytes=MX_ALIGN)
+        dst = out_rounded[:].rearrange("p (c i t) -> p c t i", i=LINE, t=PACK)
+        src = result[:].rearrange("p (t c i) -> p c t i", i=LINE, t=PACK)
+        cut = SCALAR_COLUMNS // LINE
         nc.scalar.copy(dst[:, :cut], src[:, :cut])
         nc.vector.tensor_copy(dst[:, cut:], src[:, cut:])
-        out_codes = keep.tile([P, V], I32, name="out_codes", align_bytes=64)
-        out_scales = keep.tile([P, V], U8, name="out_scales", align_bytes=64)
-        nc.vector.quantize_mx(out=out_codes[:].bitcast(FP8X4), scales=out_scales[:], in_=rounded[:])
+        out_codes = keep.tile([P, V], I32, name="out_codes", align_bytes=MX_ALIGN)
+        out_scales = keep.tile([P, V], U8, name="out_scales", align_bytes=MX_ALIGN)
+        nc.vector.quantize_mx(out=out_codes[:].bitcast(FP8X4), scales=out_scales[:], in_=out_rounded[:])
         nc.sync.dma_start(out_1[0].rearrange("p c r -> p (c r)").bitcast(I32), out_codes[:])
-        for q in range(4):
+        for q in range(QUADRANTS):
             queue = nc.scalar if q % 2 == 0 else nc.sync
             queue.dma_start(
                 out_2[0, 4 * q : 4 * q + 4, :].bitcast(I32),

@@ -62,7 +62,8 @@ def tile_picked_zmodd_tanh_po_kernel(
         before_tap2_pair1 = marks(sampled[2, 2], sampled[2, 3])
         before_tap2_pair0 = marks(sampled[2, 0], sampled[2, 1])
         before_mask0_pair1 = marks(rows[1, 2], rows[1, 3])
-        before_partials = marks(partial[1], partial[0])
+        before_mask0_pair0 = marks(rows[1, 0], rows[1, 1])
+        before_tap1_pair0 = marks(sampled[1, 0], sampled[1, 1])
 
         def load_list(name, dram):
             tile = keep.tile(list(dram.shape), U16, name=name)
@@ -152,8 +153,8 @@ def tile_picked_zmodd_tanh_po_kernel(
         def leave_y(t):
             nc.scalar.copy(rows[0, t][:], banks[0, t][:])
 
-        def leave_mask(d, t, bias=0.0):
-            nc.scalar.activation(rows[d + 1, t][:], banks[d + 1, t][:], TANH, bias=bias)
+        def leave_mask(d, t, bias=0.0, scale=1.0):
+            nc.scalar.activation(rows[d + 1, t][:], banks[d + 1, t][:], TANH, bias=bias, scale=scale)
 
         def sample(d, t):
             nc.vector.tensor_copy(sampled[d, t][:], rows[0, t][:].indirect(pos_lists[d][:]))
@@ -163,7 +164,7 @@ def tile_picked_zmodd_tanh_po_kernel(
             nc.vector.tensor_tensor(of_set(terms[d, t // 2], t % 2), gathered_mask, sampled[d, t][:], MULT)
 
         def add_first_taps(h):
-            nc.vector.tensor_tensor(partial[h][:], terms[0, h][:], terms[1, h][:], ADD)
+            nc.gpsimd.tensor_tensor(partial[h][:], terms[0, h][:], terms[1, h][:], ADD)
 
         out_rows = out_0.rearrange("(p t) v -> p t v", t=PACK)
 
@@ -187,39 +188,51 @@ def tile_picked_zmodd_tanh_po_kernel(
             sample(0, t)
         round_pair(1, 0, 0)
         multiply_pair(1, 0, 0)
-        round_pair(1, 1, 1)
+        round_pair(1, 1, 1, on_vector=True)
         sample(1, 2)
+        sample(1, 3)
         multiply_pair(1, 1, 1)
-        for t in (3, 0, 1):
-            sample(1, t)
-        round_pair(1, 1, 0, reads=before_tap2_pair1)
+        round_pair(1, 1, 0, reads=before_tap1_pair0)
+        sample(1, 0)
+        sample(1, 1)
         multiply_pair(1, 1, 0)
-        sample(2, 2)
-        sample(2, 3)
         round_pair(2, 0, 1, reads=before_mask0_pair1)
         multiply_pair(2, 0, 1)
-        round_pair(2, 0, 0, reads=before_tap2_pair0)
+        round_pair(2, 0, 0, reads=before_mask0_pair0)
         multiply_pair(2, 0, 0)
-        sample(2, 0)
-        sample(2, 1)
 
         leave_mask(0, 2)
         leave_mask(0, 3)
+        round_pair(2, 1, 0)
         round_pair(2, 1, 1, on_vector=True)
         modulate(0, 2)
         multiply_pair(2, 1, 1)
         modulate(0, 3)
-        for (w, g, h), (d, first_set) in [((2, 1, 0), (0, 0)), ((3, 0, 1), (1, 2)), ((3, 1, 1), (1, 0))]:
-            round_pair(w, g, h)
-            multiply_pair(w, g, h)
-            leave_mask(d, first_set)
-            leave_mask(d, first_set + 1)
-            modulate(d, first_set)
-            modulate(d, first_set + 1)
-        round_pair(3, 0, 0, reads=before_partials)
-        multiply_pair(3, 0, 0)
+        multiply_pair(2, 1, 0)
+        leave_mask(0, 0)
+        leave_mask(0, 1)
+        modulate(0, 0)
+        modulate(0, 1)
+        round_pair(3, 0, 1)
+        multiply_pair(3, 0, 1)
+        leave_mask(1, 2)
+        leave_mask(1, 3, *before_tap2_pair1)
+        modulate(1, 2)
+        modulate(1, 3)
         add_first_taps(1)
+        sample(2, 2)
+        sample(2, 3)
+        round_pair(3, 1, 1)
+        multiply_pair(3, 1, 1)
+        leave_mask(1, 0)
+        round_pair(3, 0, 0)
+        modulate(1, 0)
+        multiply_pair(3, 0, 0)
+        leave_mask(1, 1, *before_tap2_pair0)
+        modulate(1, 1)
         add_first_taps(0)
+        sample(2, 0)
+        sample(2, 1)
         round_pair(3, 1, 0)
         multiply_pair(3, 1, 0)
 

@@ -14,7 +14,9 @@ U8 = mybir.dt.uint8
 FP8X4 = mybir.dt.float8_e4m3fn_x4
 MULT = mybir.AluOpType.mult
 ADD = mybir.AluOpType.add
-TANH = mybir.ActivationFunctionType.Tanh
+SUB = mybir.AluOpType.subtract
+SIGMOID = mybir.ActivationFunctionType.Sigmoid
+COPY = mybir.ActivationFunctionType.Copy
 IDENTITY = mybir.ActivationFunctionType.Identity
 
 P = 128
@@ -24,7 +26,8 @@ QUADRANTS = 4
 TAPS = 3
 MX_ALIGN = 64
 LINE = 4
-SCALAR_COLUMNS = 96
+SCALAR_COLUMNS = 48
+HALF = V // 2
 
 
 def tile_picked_zmodd_tanh_po_kernel(
@@ -36,34 +39,20 @@ def tile_picked_zmodd_tanh_po_kernel(
         keep = ctx.enter_context(tc.tile_pool(name="keep", bufs=1))
         psum = ctx.enter_context(tc.psum_pool(name="psum", bufs=2))
 
-        rows = {
-            (w, t): keep.tile([P, S], F32, name="rows%d%d" % (w, t)) for w in range(len(weights)) for t in range(PACK)
-        }
-        sampled = {(d, t): keep.tile([P, V], F32, name="sampled%d%d" % (d, t)) for d in range(TAPS) for t in range(PACK)}
-        terms = {(d, h): keep.tile([P, 2 * V], F32, name="terms%d%d" % (d, h)) for d in range(TAPS) for h in range(2)}
-        partial = [keep.tile([P, 2 * V], F32, name="partial%d" % h) for h in range(2)]
         result = keep.tile([P, PACK * V], F32, name="result")
 
         def of_set(tile, t):
             return tile[:, t * V : (t + 1) * V]
 
-        def marks(first, second):
-            bias, scale = first[:, 0:1], second[:, 0:1]
-            nc.vector.memset(bias, 0.0)
-            nc.vector.memset(scale, 1.0)
-            return bias, scale
-
         zero = keep.tile([P, 1], F32, name="zero")
         nc.vector.memset(zero[:], 0.0)
-        before_sum0 = of_set(result, 0)[:, 0:1]
-        nc.scalar.activation(before_sum0, zero[:], TANH)
-        before_sum2 = of_set(result, 2)[:, 0:1]
-        nc.vector.memset(before_sum2, 0.0)
-        before_tap2_pair1 = marks(sampled[2, 2], sampled[2, 3])
-        before_tap2_pair0 = marks(sampled[2, 0], sampled[2, 1])
-        before_mask0_pair1 = marks(rows[1, 2], rows[1, 3])
-        before_mask0_pair0 = marks(rows[1, 0], rows[1, 1])
-        before_tap1_pair0 = marks(sampled[1, 0], sampled[1, 1])
+        half = keep.tile([P, 1], F32, name="half")
+        nc.scalar.activation(half[:], zero[:], SIGMOID)
+
+        early = {t: keep.tile([P, S], F32, name="rows1%d" % t, align_bytes=MX_ALIGN) for t in range(PACK)}
+        for t in range(PACK):
+            nc.vector.memset(early[t][:, 0:1], float(t % 2))
+        before_mask0 = [(early[2 * h][:, 0:1], early[2 * h + 1][:, 0:1]) for h in range(2)]
 
         def load_list(name, dram):
             tile = keep.tile(list(dram.shape), U16, name=name)
@@ -92,19 +81,19 @@ def tile_picked_zmodd_tanh_po_kernel(
                 planes[32 * q : 32 * q + 4 * PASSES, :].bitcast(I32),
                 x_scales[:, 4 * q : 4 * q + 4, :].bitcast(I32),
             )
-        load_weight(0, 0)
         words.append(load_words(1))
+        load_weight(0, 0)
         load_weight(0, 1)
         load_weight(1, 0)
         pos_lists = [load_list("pos1_list", pos1)]
         load_weight(1, 1)
-        pos_lists.append(load_list("pos2_list", pos2))
-        load_weight(2, 0)
-        pos_lists.append(load_list("pos3_list", pos3))
-        load_weight(2, 1)
         cen_list = load_list("cen_list", cen)
+        load_weight(2, 0)
+        load_weight(2, 1)
         load_weight(3, 0)
         load_weight(3, 1)
+        pos_lists.append(load_list("pos2_list", pos2))
+        pos_lists.append(load_list("pos3_list", pos3))
 
         picked = [keep.tile([P, S], U32, name="picked%d" % g, align_bytes=MX_ALIGN) for g in range(PASSES)]
         picked_scales = keep.tile([P, S], U8, name="picked_scales", align_bytes=MX_ALIGN)
@@ -115,16 +104,21 @@ def tile_picked_zmodd_tanh_po_kernel(
         rounded = {}
         banks = {}
 
-        def round_pair(w, g, h, on_vector=False, reads=None):
-            tile = keep.tile([P, 2, P, PACK], BF16, name="rounded%d%d%d" % (w, g, h), align_bytes=MX_ALIGN)
+        def round_pair(w, g, h, on_scalar=P, reads=None, tag="", on_gpsimd=False):
+            name = "rounded%d%d%d" % (w, g, h)
+            tile = keep.tile([P, 2, P, PACK], BF16, name=name, tag=tag or name, align_bytes=MX_ALIGN)
             src = raw[w, g][:].rearrange("p j (i t) -> p i j t", t=PACK)[:, :, :, 2 * h : 2 * h + 2]
             dst = tile[:].rearrange("p u i j -> p i j u")
-            if on_vector:
-                nc.vector.tensor_copy(dst, src)
-            elif reads:
-                nc.scalar.activation(dst, src, IDENTITY, bias=reads[0], scale=reads[1])
-            else:
-                nc.scalar.copy(dst, src)
+            if on_gpsimd:
+                nc.gpsimd.tensor_scalar(dst, src, 1.0, 0.0, MULT, ADD)
+                rounded[w, g, h] = tile
+                return
+            if on_scalar > 0 and reads:
+                nc.scalar.activation(dst[:, :on_scalar], src[:, :on_scalar], IDENTITY, bias=reads[0], scale=reads[1])
+            elif on_scalar > 0:
+                nc.scalar.copy(dst[:, :on_scalar], src[:, :on_scalar])
+            if on_scalar < P:
+                nc.vector.tensor_copy(dst[:, on_scalar:], src[:, on_scalar:])
             rounded[w, g, h] = tile
 
         def multiply_pair(w, g, h):
@@ -150,111 +144,177 @@ def tile_picked_zmodd_tanh_po_kernel(
                     stop=(g == PASSES - 1),
                 )
 
-        def leave_y(t):
-            nc.scalar.copy(rows[0, t][:], banks[0, t][:])
+        rows = {}
+        gates = {}
+        sampled = {}
+        terms = {}
+        partial = {}
 
-        def leave_mask(d, t, bias=0.0, scale=1.0):
-            nc.scalar.activation(rows[d + 1, t][:], banks[d + 1, t][:], TANH, bias=bias, scale=scale)
+        def pair_tile(store, key, name, tag=""):
+            if key not in store:
+                store[key] = keep.tile([P, 2 * V], F32, name=name, tag=tag, align_bytes=MX_ALIGN)
+            return store[key]
 
-        def sample(d, t):
-            nc.vector.tensor_copy(sampled[d, t][:], rows[0, t][:].indirect(pos_lists[d][:]))
+        def leave(w, t, on_vector=False, tag="", reads=None):
+            if w == 1 and t in early:
+                rows[w, t] = early[t]
+            else:
+                rows[w, t] = keep.tile([P, S], F32, name="rows%d%d" % (w, t), tag=tag or "rows%d%d" % (w, t), align_bytes=MX_ALIGN)
+            if on_vector:
+                nc.vector.tensor_copy(rows[w, t][:], banks[w, t][:])
+            elif reads:
+                nc.scalar.activation(rows[w, t][:], banks[w, t][:], IDENTITY, bias=reads[0], scale=reads[1])
+            elif w == 0:
+                nc.scalar.activation(rows[w, t][:], banks[w, t][:], COPY, scale=2.0)
+            else:
+                nc.scalar.copy(rows[w, t][:], banks[w, t][:])
 
-        def modulate(d, t):
-            gathered_mask = rows[d + 1, t][:].indirect(cen_list[:])
-            nc.vector.tensor_tensor(of_set(terms[d, t // 2], t % 2), gathered_mask, sampled[d, t][:], MULT)
+        def gate(d, t, tag=""):
+            tile = pair_tile(gates, (d, t // 2), "gates%d%d" % (d, t // 2), tag)
+            nc.scalar.activation(of_set(tile, t % 2), rows[d + 1, t][:].indirect(cen_list[:]), SIGMOID, scale=2.0)
+
+        def sample(d, t, tag=""):
+            tile = pair_tile(sampled, (d, t // 2), "sampled%d%d" % (d, t // 2), tag)
+            nc.vector.tensor_copy(of_set(tile, t % 2), rows[0, t][:].indirect(pos_lists[d][:]))
+
+        def modulate(d, h, u=None, tag=""):
+            tile = pair_tile(terms, (d, h), "terms%d%d" % (d, h), tag)
+            cols = slice(0, 2 * V) if u is None else slice(u * V, (u + 1) * V)
+            nc.vector.scalar_tensor_tensor(
+                tile[:, cols], gates[d, h][:, cols], half[:], sampled[d, h][:, cols], SUB, MULT
+            )
 
         def add_first_taps(h):
+            partial[h] = keep.tile([P, 2 * V], F32, name="partial%d" % h)
             nc.gpsimd.tensor_tensor(partial[h][:], terms[0, h][:], terms[1, h][:], ADD)
 
-        out_rows = out_0.rearrange("(p t) v -> p t v", t=PACK)
+        out_rows = out_0.rearrange("(p t) v -> p (t v)", t=PACK)
 
-        def finish(t):
-            h, u = divmod(t, 2)
-            nc.vector.tensor_tensor(of_set(result, t), of_set(partial[h], u), of_set(terms[2, h], u), ADD)
-            nc.sync.dma_start(out_rows[:, t, :], of_set(result, t))
+        def finish(h, u=None):
+            part = slice(0, 2 * V) if u is None else slice(u * V, (u + 1) * V)
+            cols = slice(2 * h * V + part.start, 2 * h * V + part.stop)
+            nc.vector.tensor_tensor(result[:, cols], partial[h][:, part], terms[2, h][:, part], ADD)
+            if u is None:
+                nc.sync.dma_start(out_rows[:, cols], result[:, cols])
 
-        for g in range(PASSES):
-            round_pair(0, g, 1, on_vector=True)
-            round_pair(0, g, 0)
-            multiply_pair(0, g, 1)
-            multiply_pair(0, g, 0)
-        for t in (2, 3, 0, 1):
-            leave_y(t)
+        def mask_pair(d, h):
+            leave(d + 1, 2 * h)
+            leave(d + 1, 2 * h + 1)
+            gate(d, 2 * h)
+            gate(d, 2 * h + 1)
 
-        round_pair(1, 0, 1, on_vector=True)
-        sample(0, 2)
+        round_pair(0, 0, 1)
+        round_pair(0, 0, 0, on_scalar=0)
+        multiply_pair(0, 0, 0)
+        multiply_pair(0, 0, 1)
+        round_pair(0, 1, 1, on_scalar=0)
+        round_pair(0, 1, 0)
+        multiply_pair(0, 1, 1)
+        multiply_pair(0, 1, 0)
+        leave(0, 2)
+        leave(0, 3)
+        leave(0, 0)
+        leave(0, 1)
+        round_pair(1, 0, 1, on_scalar=0)
+        round_pair(1, 0, 0, on_scalar=0)
         multiply_pair(1, 0, 1)
-        for t in (3, 0, 1):
-            sample(0, t)
-        round_pair(1, 0, 0)
         multiply_pair(1, 0, 0)
-        round_pair(1, 1, 1, on_vector=True)
+        sample(0, 2)
+        sample(0, 3)
+        sample(0, 0)
+        sample(0, 1)
+        round_pair(1, 1, 1)
+        round_pair(1, 1, 0, on_scalar=84)
+        multiply_pair(1, 1, 1)
+        multiply_pair(1, 1, 0)
+        round_pair(2, 0, 1, on_scalar=0)
+        round_pair(2, 0, 0, on_scalar=96, reads=before_mask0[1])
+        multiply_pair(2, 0, 1)
+        multiply_pair(2, 0, 0)
+        leave(1, 2, reads=before_mask0[0])
+        leave(1, 3)
+        gate(0, 2)
+        gate(0, 3)
+        leave(1, 0)
+        leave(1, 1)
+        gate(0, 0)
+        gate(0, 1)
+        round_pair(2, 1, 1, on_scalar=0)
+        round_pair(2, 1, 0, on_scalar=0)
+        multiply_pair(2, 1, 1)
+        multiply_pair(2, 1, 0)
+        modulate(0, 1, tag="rounded211")
+        round_pair(3, 0, 1, on_scalar=0)
+        round_pair(3, 0, 0, on_scalar=0)
+        multiply_pair(3, 0, 1)
+        multiply_pair(3, 0, 0)
+        modulate(0, 0, tag="rounded301")
+        leave(2, 2)
+        leave(2, 3)
+        gate(1, 2)
+        gate(1, 3)
+        leave(2, 0)
+        leave(2, 1)
+        gate(1, 0)
+        gate(1, 1)
+        round_pair(3, 1, 1, on_scalar=0)
+        round_pair(3, 1, 0, on_scalar=0)
+        multiply_pair(3, 1, 1)
+        multiply_pair(3, 1, 0)
         sample(1, 2)
         sample(1, 3)
-        multiply_pair(1, 1, 1)
-        round_pair(1, 1, 0, reads=before_tap1_pair0)
         sample(1, 0)
         sample(1, 1)
-        multiply_pair(1, 1, 0)
-        round_pair(2, 0, 1, reads=before_mask0_pair1)
-        multiply_pair(2, 0, 1)
-        round_pair(2, 0, 0, reads=before_mask0_pair0)
-        multiply_pair(2, 0, 0)
-
-        leave_mask(0, 2)
-        leave_mask(0, 3)
-        round_pair(2, 1, 0)
-        round_pair(2, 1, 1, on_vector=True)
-        modulate(0, 2)
-        multiply_pair(2, 1, 1)
-        modulate(0, 3)
-        multiply_pair(2, 1, 0)
-        leave_mask(0, 0)
-        leave_mask(0, 1)
-        modulate(0, 0)
-        modulate(0, 1)
-        round_pair(3, 0, 1)
-        multiply_pair(3, 0, 1)
-        leave_mask(1, 2)
-        leave_mask(1, 3, *before_tap2_pair1)
-        modulate(1, 2)
-        modulate(1, 3)
+        modulate(1, 1)
+        modulate(1, 0)
         add_first_taps(1)
+        add_first_taps(0)
         sample(2, 2)
         sample(2, 3)
-        round_pair(3, 1, 1)
-        multiply_pair(3, 1, 1)
-        leave_mask(1, 0)
-        round_pair(3, 0, 0)
-        modulate(1, 0)
-        multiply_pair(3, 0, 0)
-        leave_mask(1, 1, *before_tap2_pair0)
-        modulate(1, 1)
-        add_first_taps(0)
         sample(2, 0)
         sample(2, 1)
-        round_pair(3, 1, 0)
-        multiply_pair(3, 1, 0)
-
-        leave_mask(2, 2)
-        leave_mask(2, 3, bias=before_sum2)
-        leave_mask(2, 0)
-        leave_mask(2, 1, bias=before_sum0)
-        for first_set in (2, 0):
-            modulate(2, first_set)
-            modulate(2, first_set + 1)
-            finish(first_set)
-            finish(first_set + 1)
+        leave(3, 2)
+        leave(3, 3)
+        gate(2, 2)
+        gate(2, 3)
+        leave(3, 0)
+        leave(3, 1)
+        gate(2, 0)
+        gate(2, 1)
+        modulate(2, 1)
 
         out_rounded = keep.tile([P, V * PACK], BF16, name="out_rounded", align_bytes=MX_ALIGN)
-        dst = out_rounded[:].rearrange("p (c i t) -> p c t i", i=LINE, t=PACK)
-        src = result[:].rearrange("p (t c i) -> p c t i", i=LINE, t=PACK)
-        cut = SCALAR_COLUMNS // LINE
-        nc.scalar.copy(dst[:, :cut], src[:, :cut])
-        nc.vector.tensor_copy(dst[:, cut:], src[:, cut:])
         out_codes = keep.tile([P, V], I32, name="out_codes", align_bytes=MX_ALIGN)
         out_scales = keep.tile([P, V], U8, name="out_scales", align_bytes=MX_ALIGN)
-        nc.vector.quantize_mx(out=out_codes[:].bitcast(FP8X4), scales=out_scales[:], in_=out_rounded[:])
+        dst = out_rounded[:].rearrange("p (c i t) -> p c t i", i=LINE, t=PACK)
+        src = result[:].rearrange("p (t c i) -> p c t i", i=LINE, t=PACK)
+        def round_half(a, scalar_columns):
+            lo, hi = a * HALF // LINE, (a + 1) * HALF // LINE
+            cut = lo + scalar_columns // LINE
+            if cut > lo:
+                nc.scalar.copy(dst[:, lo:cut], src[:, lo:cut])
+            nc.vector.tensor_copy(dst[:, cut:hi], src[:, cut:hi])
+
+        def quantise_half(a):
+            s = slice(a * HALF, (a + 1) * HALF)
+            nc.vector.quantize_mx(
+                out=out_codes[:, s].bitcast(FP8X4),
+                scales=out_scales[:, s],
+                in_=out_rounded[:, PACK * s.start : PACK * s.stop],
+            )
+
+        modulate(2, 0, 0)
+        finish(1)
+        modulate(2, 0, 1)
+        finish(0, 0)
+        for a in range(2):
+            part = slice(V + a * HALF, V + (a + 1) * HALF)
+            nc.vector.tensor_tensor(result[:, part], partial[0][:, part], terms[2, 0][:, part], ADD)
+        nc.sync.dma_start(out_rows[:, 0 : 2 * V], result[:, 0 : 2 * V])
+        for a in range(2):
+            round_half(a, SCALAR_COLUMNS)
+        for a in range(2):
+            quantise_half(a)
         nc.sync.dma_start(out_1[0].rearrange("p c r -> p (c r)").bitcast(I32), out_codes[:])
         for q in range(QUADRANTS):
             queue = nc.scalar if q % 2 == 0 else nc.sync

@@ -39,6 +39,9 @@ def tile_picked_zmodd_tanh_po_kernel(
         keep = ctx.enter_context(tc.tile_pool(name="keep", bufs=1))
         psum = ctx.enter_context(tc.psum_pool(name="psum", bufs=2))
 
+        planes = keep.tile([P, T], U8, name="planes", align_bytes=MX_ALIGN)
+        nc.vector.memset(planes[:].bitcast(I32), 0)
+
         result = keep.tile([P, PACK * V], F32, name="result")
 
         def of_set(tile, t):
@@ -70,9 +73,6 @@ def tile_picked_zmodd_tanh_po_kernel(
             raw[w, g] = keep.tile([P, PACK, N], F32, name="raw%d%d" % (w, g))
             k_rows = weights[w][g * P * PACK : (g + 1) * P * PACK, :]
             nc.sync.dma_start(raw[w, g][:], k_rows.rearrange("(p j) m -> p j m", j=PACK))
-
-        planes = keep.tile([P, T], U8, name="planes", align_bytes=MX_ALIGN)
-        nc.gpsimd.memset(planes[:].bitcast(I32), 0)
 
         words = [load_words(0)]
         offs_list = load_list("offs_list", offs)
@@ -122,8 +122,8 @@ def tile_picked_zmodd_tanh_po_kernel(
             rounded[w, g, h] = tile
 
         def multiply_pair(w, g, h):
-            codes = keep.tile([P, 2 * P], U32, name="codes%d%d%d" % (w, g, h), align_bytes=MX_ALIGN)
-            scales = keep.tile([P, 2 * P], U8, name="scales%d%d%d" % (w, g, h), align_bytes=MX_ALIGN)
+            codes = keep.tile([P, 2 * P], U32, name="codes%d%d%d" % (w, g, h), tag="codes%d%d%d" % (w, g, h), align_bytes=MX_ALIGN)
+            scales = keep.tile([P, 2 * P], U8, name="scales%d%d%d" % (w, g, h), tag="scales%d%d%d" % (w, g, h), align_bytes=MX_ALIGN)
             nc.vector.quantize_mx(
                 out=codes[:].bitcast(FP8X4),
                 scales=scales[:],
@@ -149,11 +149,18 @@ def tile_picked_zmodd_tanh_po_kernel(
         sampled = {}
         terms = {}
         partial = {}
+        whole_terms = {}
 
         def pair_tile(store, key, name, tag=""):
             if key not in store:
                 store[key] = keep.tile([P, 2 * V], F32, name=name, tag=tag, align_bytes=MX_ALIGN)
             return store[key]
+
+        def term_pair(d, h, tag=""):
+            if d not in whole_terms:
+                whole_terms[d] = keep.tile([P, PACK * V], F32, name="terms%d" % d, tag=tag, align_bytes=MX_ALIGN)
+            terms[d, h] = whole_terms[d][:, 2 * h * V : 2 * (h + 1) * V]
+            return terms[d, h]
 
         def leave(w, t, on_vector=False, tag="", reads=None):
             if w == 1 and t in early:
@@ -178,15 +185,17 @@ def tile_picked_zmodd_tanh_po_kernel(
             nc.vector.tensor_copy(of_set(tile, t % 2), rows[0, t][:].indirect(pos_lists[d][:]))
 
         def modulate(d, h, u=None, tag=""):
-            tile = pair_tile(terms, (d, h), "terms%d%d" % (d, h), tag)
+            tile = term_pair(d, h, tag)
             cols = slice(0, 2 * V) if u is None else slice(u * V, (u + 1) * V)
             nc.vector.scalar_tensor_tensor(
                 tile[:, cols], gates[d, h][:, cols], half[:], sampled[d, h][:, cols], SUB, MULT
             )
 
-        def add_first_taps(h):
-            partial[h] = keep.tile([P, 2 * V], F32, name="partial%d" % h)
-            nc.gpsimd.tensor_tensor(partial[h][:], terms[0, h][:], terms[1, h][:], ADD)
+        def add_first_taps():
+            both = keep.tile([P, PACK * V], F32, name="partial")
+            nc.gpsimd.tensor_tensor(both[:], whole_terms[0][:], whole_terms[1][:], ADD)
+            for h in range(2):
+                partial[h] = both[:, 2 * h * V : 2 * (h + 1) * V]
 
         out_rows = out_0.rearrange("(p t) v -> p (t v)", t=PACK)
 
@@ -202,6 +211,12 @@ def tile_picked_zmodd_tanh_po_kernel(
             leave(d + 1, 2 * h + 1)
             gate(d, 2 * h)
             gate(d, 2 * h + 1)
+
+        def modulate_on_gpsimd(d, h, tag):
+            centred = keep.tile([P, 2 * V], F32, name="centred%d%d" % (d, h), tag=tag, align_bytes=MX_ALIGN)
+            nc.gpsimd.tensor_scalar(centred[:], gates[d, h][:], 1.0, -0.5, MULT, ADD)
+            tile = term_pair(d, h)
+            nc.gpsimd.tensor_tensor(tile, centred[:], sampled[d, h][:], MULT)
 
         round_pair(0, 0, 1)
         round_pair(0, 0, 0, on_scalar=0)
@@ -248,7 +263,6 @@ def tile_picked_zmodd_tanh_po_kernel(
         round_pair(3, 0, 0, on_scalar=0)
         multiply_pair(3, 0, 1)
         multiply_pair(3, 0, 0)
-        modulate(0, 0, tag="rounded301")
         leave(2, 2)
         leave(2, 3)
         gate(1, 2)
@@ -261,14 +275,14 @@ def tile_picked_zmodd_tanh_po_kernel(
         round_pair(3, 1, 0, on_scalar=0)
         multiply_pair(3, 1, 1)
         multiply_pair(3, 1, 0)
+        modulate_on_gpsimd(0, 0, "rounded311")
         sample(1, 2)
         sample(1, 3)
         sample(1, 0)
         sample(1, 1)
         modulate(1, 1)
         modulate(1, 0)
-        add_first_taps(1)
-        add_first_taps(0)
+        add_first_taps()
         sample(2, 2)
         sample(2, 3)
         sample(2, 0)
@@ -281,7 +295,8 @@ def tile_picked_zmodd_tanh_po_kernel(
         leave(3, 1)
         gate(2, 0)
         gate(2, 1)
-        modulate(2, 1)
+        modulate(2, 1, 0)
+        modulate(2, 1, 1)
 
         out_rounded = keep.tile([P, V * PACK], BF16, name="out_rounded", align_bytes=MX_ALIGN)
         out_codes = keep.tile([P, V], I32, name="out_codes", align_bytes=MX_ALIGN)
@@ -303,8 +318,10 @@ def tile_picked_zmodd_tanh_po_kernel(
                 in_=out_rounded[:, PACK * s.start : PACK * s.stop],
             )
 
+        finish(1, 0)
+        finish(1, 1)
+        nc.sync.dma_start(out_rows[:, 2 * V : 4 * V], result[:, 2 * V : 4 * V])
         modulate(2, 0, 0)
-        finish(1)
         modulate(2, 0, 1)
         finish(0, 0)
         for a in range(2):

@@ -14,7 +14,7 @@ U8 = mybir.dt.uint8
 FP8X4 = mybir.dt.float8_e4m3fn_x4
 MULT = mybir.AluOpType.mult
 ADD = mybir.AluOpType.add
-SUB = mybir.AluOpType.subtract
+SUBTRACT = mybir.AluOpType.subtract
 SIGMOID = mybir.ActivationFunctionType.Sigmoid
 COPY = mybir.ActivationFunctionType.Copy
 IDENTITY = mybir.ActivationFunctionType.Identity
@@ -23,11 +23,15 @@ P = 128
 PACK = 4
 PASSES = K // (P * PACK)
 QUADRANTS = 4
-TAPS = 3
 MX_ALIGN = 64
 LINE = 4
-SCALAR_COLUMNS = 48
 HALF = V // 2
+PAIRS = (1, 0)
+SETS = (2, 3, 0, 1)
+
+SCALAR_SHARE_W1 = 104
+SCALAR_SHARE_W2 = 80
+SCALAR_SHARE_OUT = (48, 32)
 
 
 def tile_picked_zmodd_tanh_po_kernel(
@@ -39,23 +43,31 @@ def tile_picked_zmodd_tanh_po_kernel(
         keep = ctx.enter_context(tc.tile_pool(name="keep", bufs=1))
         psum = ctx.enter_context(tc.psum_pool(name="psum", bufs=2))
 
-        planes = keep.tile([P, T], U8, name="planes", align_bytes=MX_ALIGN)
-        nc.vector.memset(planes[:].bitcast(I32), 0)
-
-        result = keep.tile([P, PACK * V], F32, name="result")
+        def float_tile(columns, name, tag=""):
+            return keep.tile([P, columns], F32, name=name, tag=tag, align_bytes=MX_ALIGN)
 
         def of_set(tile, t):
             return tile[:, t * V : (t + 1) * V]
 
+        def of_pair(tile, h):
+            return tile[:, 2 * h * V : 2 * (h + 1) * V]
+
+        planes = keep.tile([P, T], U8, name="planes", align_bytes=MX_ALIGN)
+        nc.vector.memset(planes[:].bitcast(I32), 0)
+
         zero = keep.tile([P, 1], F32, name="zero")
         nc.vector.memset(zero[:], 0.0)
-        half = keep.tile([P, 1], F32, name="half")
-        nc.scalar.activation(half[:], zero[:], SIGMOID)
+        one_half = keep.tile([P, 1], F32, name="one_half")
+        nc.scalar.activation(one_half[:], zero[:], SIGMOID)
 
-        early = {t: keep.tile([P, S], F32, name="rows1%d" % t, align_bytes=MX_ALIGN) for t in range(PACK)}
+        rows = {(1, t): float_tile(S, "rows1%d" % t) for t in range(PACK)}
+
         for t in range(PACK):
-            nc.vector.memset(early[t][:, 0:1], float(t % 2))
-        before_mask0 = [(early[2 * h][:, 0:1], early[2 * h + 1][:, 0:1]) for h in range(2)]
+            nc.vector.memset(rows[1, t][:, 0:1], float(t % 2))
+        marks_of_mask0 = [(rows[1, 2 * h][:, 0:1], rows[1, 2 * h + 1][:, 0:1]) for h in range(2)]
+
+        def rounded_tag(w, g, h):
+            return "rounded%d%d%d" % (w, g, h)
 
         def load_list(name, dram):
             tile = keep.tile(list(dram.shape), U16, name=name)
@@ -88,10 +100,9 @@ def tile_picked_zmodd_tanh_po_kernel(
         pos_lists = [load_list("pos1_list", pos1)]
         load_weight(1, 1)
         cen_list = load_list("cen_list", cen)
-        load_weight(2, 0)
-        load_weight(2, 1)
-        load_weight(3, 0)
-        load_weight(3, 1)
+        for w in (2, 3):
+            for g in range(PASSES):
+                load_weight(w, g)
         pos_lists.append(load_list("pos2_list", pos2))
         pos_lists.append(load_list("pos3_list", pos3))
 
@@ -103,27 +114,28 @@ def tile_picked_zmodd_tanh_po_kernel(
 
         rounded = {}
         banks = {}
+        gates = {}
+        sampled = {}
+        terms = {}
 
-        def round_pair(w, g, h, on_scalar=P, reads=None, tag="", on_gpsimd=False):
-            name = "rounded%d%d%d" % (w, g, h)
-            tile = keep.tile([P, 2, P, PACK], BF16, name=name, tag=tag or name, align_bytes=MX_ALIGN)
+        def round_pair(w, g, h, scalar_share, marks=None):
+            tag = rounded_tag(w, g, h)
+            tile = keep.tile([P, 2, P, PACK], BF16, name=tag, tag=tag, align_bytes=MX_ALIGN)
             src = raw[w, g][:].rearrange("p j (i t) -> p i j t", t=PACK)[:, :, :, 2 * h : 2 * h + 2]
             dst = tile[:].rearrange("p u i j -> p i j u")
-            if on_gpsimd:
-                nc.gpsimd.tensor_scalar(dst, src, 1.0, 0.0, MULT, ADD)
-                rounded[w, g, h] = tile
-                return
-            if on_scalar > 0 and reads:
-                nc.scalar.activation(dst[:, :on_scalar], src[:, :on_scalar], IDENTITY, bias=reads[0], scale=reads[1])
-            elif on_scalar > 0:
-                nc.scalar.copy(dst[:, :on_scalar], src[:, :on_scalar])
-            if on_scalar < P:
-                nc.vector.tensor_copy(dst[:, on_scalar:], src[:, on_scalar:])
+            if marks:
+                nc.scalar.activation(
+                    dst[:, :scalar_share], src[:, :scalar_share], IDENTITY, bias=marks[0], scale=marks[1]
+                )
+            elif scalar_share > 0:
+                nc.scalar.copy(dst[:, :scalar_share], src[:, :scalar_share])
+            if scalar_share < P:
+                nc.vector.tensor_copy(dst[:, scalar_share:], src[:, scalar_share:])
             rounded[w, g, h] = tile
 
         def multiply_pair(w, g, h):
-            codes = keep.tile([P, 2 * P], U32, name="codes%d%d%d" % (w, g, h), tag="codes%d%d%d" % (w, g, h), align_bytes=MX_ALIGN)
-            scales = keep.tile([P, 2 * P], U8, name="scales%d%d%d" % (w, g, h), tag="scales%d%d%d" % (w, g, h), align_bytes=MX_ALIGN)
+            codes = keep.tile([P, 2 * P], U32, name="codes%d%d%d" % (w, g, h), align_bytes=MX_ALIGN)
+            scales = keep.tile([P, 2 * P], U8, name="scales%d%d%d" % (w, g, h), align_bytes=MX_ALIGN)
             nc.vector.quantize_mx(
                 out=codes[:].bitcast(FP8X4),
                 scales=scales[:],
@@ -144,194 +156,119 @@ def tile_picked_zmodd_tanh_po_kernel(
                     stop=(g == PASSES - 1),
                 )
 
-        rows = {}
-        gates = {}
-        sampled = {}
-        terms = {}
-        partial = {}
-        whole_terms = {}
+        def pass_on_vector(w, g):
+            for h in PAIRS:
+                round_pair(w, g, h, 0)
+            for h in PAIRS:
+                multiply_pair(w, g, h)
 
-        def pair_tile(store, key, name, tag=""):
-            if key not in store:
-                store[key] = keep.tile([P, 2 * V], F32, name=name, tag=tag, align_bytes=MX_ALIGN)
-            return store[key]
+        def leave_y(t):
+            rows[0, t] = float_tile(S, "rows0%d" % t)
+            nc.scalar.activation(rows[0, t][:], banks[0, t][:], COPY, scale=2.0)
 
-        def term_pair(d, h, tag=""):
-            if d not in whole_terms:
-                whole_terms[d] = keep.tile([P, PACK * V], F32, name="terms%d" % d, tag=tag, align_bytes=MX_ALIGN)
-            terms[d, h] = whole_terms[d][:, 2 * h * V : 2 * (h + 1) * V]
-            return terms[d, h]
+        def gate_pair(d, h, marks=None):
+            w = d + 1
+            for t in (2 * h, 2 * h + 1):
+                if (w, t) not in rows:
+                    rows[w, t] = float_tile(S, "rows%d%d" % (w, t))
+                if marks and t == 2 * h:
+                    nc.scalar.activation(rows[w, t][:], banks[w, t][:], IDENTITY, bias=marks[0], scale=marks[1])
+                else:
+                    nc.scalar.copy(rows[w, t][:], banks[w, t][:])
+            gates[d, h] = float_tile(2 * V, "gates%d%d" % (d, h))
+            for u in range(2):
+                gathered_sums = rows[w, 2 * h + u][:].indirect(cen_list[:])
+                nc.scalar.activation(of_set(gates[d, h], u), gathered_sums, SIGMOID, scale=2.0)
 
-        def leave(w, t, on_vector=False, tag="", reads=None):
-            if w == 1 and t in early:
-                rows[w, t] = early[t]
-            else:
-                rows[w, t] = keep.tile([P, S], F32, name="rows%d%d" % (w, t), tag=tag or "rows%d%d" % (w, t), align_bytes=MX_ALIGN)
-            if on_vector:
-                nc.vector.tensor_copy(rows[w, t][:], banks[w, t][:])
-            elif reads:
-                nc.scalar.activation(rows[w, t][:], banks[w, t][:], IDENTITY, bias=reads[0], scale=reads[1])
-            elif w == 0:
-                nc.scalar.activation(rows[w, t][:], banks[w, t][:], COPY, scale=2.0)
-            else:
-                nc.scalar.copy(rows[w, t][:], banks[w, t][:])
+        def sample_tap(d):
+            for h in PAIRS:
+                sampled[d, h] = float_tile(2 * V, "sampled%d%d" % (d, h))
+                for u in range(2):
+                    nc.vector.tensor_copy(of_set(sampled[d, h], u), rows[0, 2 * h + u][:].indirect(pos_lists[d][:]))
 
-        def gate(d, t, tag=""):
-            tile = pair_tile(gates, (d, t // 2), "gates%d%d" % (d, t // 2), tag)
-            nc.scalar.activation(of_set(tile, t % 2), rows[d + 1, t][:].indirect(cen_list[:]), SIGMOID, scale=2.0)
+        def modulate(out, gate, sample):
+            nc.vector.scalar_tensor_tensor(out, gate, one_half[:], sample, SUBTRACT, MULT)
 
-        def sample(d, t, tag=""):
-            tile = pair_tile(sampled, (d, t // 2), "sampled%d%d" % (d, t // 2), tag)
-            nc.vector.tensor_copy(of_set(tile, t % 2), rows[0, t][:].indirect(pos_lists[d][:]))
-
-        def modulate(d, h, u=None, tag=""):
-            tile = term_pair(d, h, tag)
-            cols = slice(0, 2 * V) if u is None else slice(u * V, (u + 1) * V)
-            nc.vector.scalar_tensor_tensor(
-                tile[:, cols], gates[d, h][:, cols], half[:], sampled[d, h][:, cols], SUB, MULT
-            )
-
-        def add_first_taps():
-            both = keep.tile([P, PACK * V], F32, name="partial")
-            nc.gpsimd.tensor_tensor(both[:], whole_terms[0][:], whole_terms[1][:], ADD)
-            for h in range(2):
-                partial[h] = both[:, 2 * h * V : 2 * (h + 1) * V]
-
-        out_rows = out_0.rearrange("(p t) v -> p (t v)", t=PACK)
-
-        def finish(h, u=None):
-            part = slice(0, 2 * V) if u is None else slice(u * V, (u + 1) * V)
-            cols = slice(2 * h * V + part.start, 2 * h * V + part.stop)
-            nc.vector.tensor_tensor(result[:, cols], partial[h][:, part], terms[2, h][:, part], ADD)
-            if u is None:
-                nc.sync.dma_start(out_rows[:, cols], result[:, cols])
-
-        def mask_pair(d, h):
-            leave(d + 1, 2 * h)
-            leave(d + 1, 2 * h + 1)
-            gate(d, 2 * h)
-            gate(d, 2 * h + 1)
-
-        def modulate_on_gpsimd(d, h, tag):
-            centred = keep.tile([P, 2 * V], F32, name="centred%d%d" % (d, h), tag=tag, align_bytes=MX_ALIGN)
-            nc.gpsimd.tensor_scalar(centred[:], gates[d, h][:], 1.0, -0.5, MULT, ADD)
-            tile = term_pair(d, h)
-            nc.gpsimd.tensor_tensor(tile, centred[:], sampled[d, h][:], MULT)
-
-        round_pair(0, 0, 1)
-        round_pair(0, 0, 0, on_scalar=0)
+        round_pair(0, 0, 1, P)
+        round_pair(0, 0, 0, 0)
         multiply_pair(0, 0, 0)
         multiply_pair(0, 0, 1)
-        round_pair(0, 1, 1, on_scalar=0)
-        round_pair(0, 1, 0)
-        multiply_pair(0, 1, 1)
-        multiply_pair(0, 1, 0)
-        leave(0, 2)
-        leave(0, 3)
-        leave(0, 0)
-        leave(0, 1)
-        round_pair(1, 0, 1, on_scalar=0)
-        round_pair(1, 0, 0, on_scalar=0)
-        multiply_pair(1, 0, 1)
-        multiply_pair(1, 0, 0)
-        sample(0, 2)
-        sample(0, 3)
-        sample(0, 0)
-        sample(0, 1)
-        round_pair(1, 1, 1)
-        round_pair(1, 1, 0, on_scalar=84)
-        multiply_pair(1, 1, 1)
-        multiply_pair(1, 1, 0)
-        round_pair(2, 0, 1, on_scalar=0)
-        round_pair(2, 0, 0, on_scalar=96, reads=before_mask0[1])
-        multiply_pair(2, 0, 1)
-        multiply_pair(2, 0, 0)
-        leave(1, 2, reads=before_mask0[0])
-        leave(1, 3)
-        gate(0, 2)
-        gate(0, 3)
-        leave(1, 0)
-        leave(1, 1)
-        gate(0, 0)
-        gate(0, 1)
-        round_pair(2, 1, 1, on_scalar=0)
-        round_pair(2, 1, 0, on_scalar=0)
-        multiply_pair(2, 1, 1)
-        multiply_pair(2, 1, 0)
-        modulate(0, 1, tag="rounded211")
-        round_pair(3, 0, 1, on_scalar=0)
-        round_pair(3, 0, 0, on_scalar=0)
-        multiply_pair(3, 0, 1)
-        multiply_pair(3, 0, 0)
-        leave(2, 2)
-        leave(2, 3)
-        gate(1, 2)
-        gate(1, 3)
-        leave(2, 0)
-        leave(2, 1)
-        gate(1, 0)
-        gate(1, 1)
-        round_pair(3, 1, 1, on_scalar=0)
-        round_pair(3, 1, 0, on_scalar=0)
-        multiply_pair(3, 1, 1)
-        multiply_pair(3, 1, 0)
-        modulate_on_gpsimd(0, 0, "rounded311")
-        sample(1, 2)
-        sample(1, 3)
-        sample(1, 0)
-        sample(1, 1)
-        modulate(1, 1)
-        modulate(1, 0)
-        add_first_taps()
-        sample(2, 2)
-        sample(2, 3)
-        sample(2, 0)
-        sample(2, 1)
-        leave(3, 2)
-        leave(3, 3)
-        gate(2, 2)
-        gate(2, 3)
-        leave(3, 0)
-        leave(3, 1)
-        gate(2, 0)
-        gate(2, 1)
-        modulate(2, 1, 0)
-        modulate(2, 1, 1)
+        round_pair(0, 1, 1, 0)
+        round_pair(0, 1, 0, P)
+        for h in PAIRS:
+            multiply_pair(0, 1, h)
+        for t in SETS:
+            leave_y(t)
+
+        pass_on_vector(1, 0)
+        sample_tap(0)
+        round_pair(1, 1, 1, P)
+        round_pair(1, 1, 0, SCALAR_SHARE_W1)
+        for h in PAIRS:
+            multiply_pair(1, 1, h)
+        round_pair(2, 0, 1, 0)
+        round_pair(2, 0, 0, SCALAR_SHARE_W2, marks=marks_of_mask0[1])
+        for h in PAIRS:
+            multiply_pair(2, 0, h)
+        gate_pair(0, 1, marks=marks_of_mask0[0])
+        gate_pair(0, 0)
+
+        pass_on_vector(2, 1)
+        terms[0] = float_tile(PACK * V, "terms0", tag=rounded_tag(2, 1, 1))
+        modulate(of_pair(terms[0], 1), gates[0, 1][:], sampled[0, 1][:])
+        pass_on_vector(3, 0)
+        for h in PAIRS:
+            gate_pair(1, h)
+        pass_on_vector(3, 1)
+
+        centred = float_tile(2 * V, "centred", tag=rounded_tag(3, 1, 1))
+        nc.gpsimd.tensor_scalar(centred[:], gates[0, 0][:], 1.0, -0.5, MULT, ADD)
+        nc.gpsimd.tensor_tensor(of_pair(terms[0], 0), centred[:], sampled[0, 0][:], MULT)
+        sample_tap(1)
+        terms[1] = float_tile(PACK * V, "terms1")
+        for h in PAIRS:
+            modulate(of_pair(terms[1], h), gates[1, h][:], sampled[1, h][:])
+        partial = keep.tile([P, PACK * V], F32, name="partial")
+        nc.gpsimd.tensor_tensor(partial[:], terms[0][:], terms[1][:], ADD)
+        sample_tap(2)
+
+        for h in PAIRS:
+            gate_pair(2, h)
+        terms[2] = float_tile(PACK * V, "terms2")
+        for t in SETS:
+            h, u = divmod(t, 2)
+            modulate(of_set(terms[2], t), of_set(gates[2, h], u), of_set(sampled[2, h], u))
+
+        result = keep.tile([P, PACK * V], F32, name="result")
+        out_rows = out_0.rearrange("(p t) v -> p (t v)", t=PACK)
+
+        def half_of_pair0(tile, a):
+            return of_pair(tile, 0).rearrange("p (u v) -> p u v", u=2)[:, :, a * HALF : (a + 1) * HALF]
+
+        for t in (2, 3):
+            nc.vector.tensor_tensor(of_set(result, t), of_set(partial, t), of_set(terms[2], t), ADD)
+        nc.sync.dma_start(of_pair(out_rows, 1), of_pair(result, 1))
+        for a in range(2):
+            nc.vector.tensor_tensor(half_of_pair0(result, a), half_of_pair0(partial, a), half_of_pair0(terms[2], a), ADD)
+        nc.sync.dma_start(of_pair(out_rows, 0), of_pair(result, 0))
 
         out_rounded = keep.tile([P, V * PACK], BF16, name="out_rounded", align_bytes=MX_ALIGN)
         out_codes = keep.tile([P, V], I32, name="out_codes", align_bytes=MX_ALIGN)
         out_scales = keep.tile([P, V], U8, name="out_scales", align_bytes=MX_ALIGN)
         dst = out_rounded[:].rearrange("p (c i t) -> p c t i", i=LINE, t=PACK)
         src = result[:].rearrange("p (t c i) -> p c t i", i=LINE, t=PACK)
-        def round_half(a, scalar_columns):
-            lo, hi = a * HALF // LINE, (a + 1) * HALF // LINE
-            cut = lo + scalar_columns // LINE
-            if cut > lo:
-                nc.scalar.copy(dst[:, lo:cut], src[:, lo:cut])
-            nc.vector.tensor_copy(dst[:, cut:hi], src[:, cut:hi])
-
-        def quantise_half(a):
-            s = slice(a * HALF, (a + 1) * HALF)
+        for a in range(2):
+            first, last = a * HALF // LINE, (a + 1) * HALF // LINE
+            cut = first + SCALAR_SHARE_OUT[a] // LINE
+            nc.scalar.copy(dst[:, first:cut], src[:, first:cut])
+            nc.vector.tensor_copy(dst[:, cut:last], src[:, cut:last])
+        for a in range(2):
+            columns = slice(a * HALF, (a + 1) * HALF)
             nc.vector.quantize_mx(
-                out=out_codes[:, s].bitcast(FP8X4),
-                scales=out_scales[:, s],
-                in_=out_rounded[:, PACK * s.start : PACK * s.stop],
+                out=out_codes[:, columns].bitcast(FP8X4),
+                scales=out_scales[:, columns],
+                in_=out_rounded[:, PACK * columns.start : PACK * columns.stop],
             )
-
-        finish(1, 0)
-        finish(1, 1)
-        nc.sync.dma_start(out_rows[:, 2 * V : 4 * V], result[:, 2 * V : 4 * V])
-        modulate(2, 0, 0)
-        modulate(2, 0, 1)
-        finish(0, 0)
-        for a in range(2):
-            part = slice(V + a * HALF, V + (a + 1) * HALF)
-            nc.vector.tensor_tensor(result[:, part], partial[0][:, part], terms[2, 0][:, part], ADD)
-        nc.sync.dma_start(out_rows[:, 0 : 2 * V], result[:, 0 : 2 * V])
-        for a in range(2):
-            round_half(a, SCALAR_COLUMNS)
-        for a in range(2):
-            quantise_half(a)
         nc.sync.dma_start(out_1[0].rearrange("p c r -> p (c r)").bitcast(I32), out_codes[:])
         for q in range(QUADRANTS):
             queue = nc.scalar if q % 2 == 0 else nc.sync

@@ -52,7 +52,7 @@ def tile_picked_zmodd_tanh_po_kernel(
         def of_pair(tile, h):
             return tile[:, 2 * h * V : 2 * (h + 1) * V]
 
-        planes = keep.tile([P, T], U8, name="planes", align_bytes=MX_ALIGN)
+        planes = keep.tile([P, PASSES * T], U8, name="planes", align_bytes=MX_ALIGN)
         nc.vector.memset(planes[:].bitcast(I32), 0)
 
         zero = keep.tile([P, 1], F32, name="zero")
@@ -90,11 +90,11 @@ def tile_picked_zmodd_tanh_po_kernel(
         offs_list = load_list("offs_list", offs)
         for q in range(QUADRANTS):
             nc.sync.dma_start(
-                planes[32 * q : 32 * q + 4 * PASSES, :].bitcast(I32),
-                x_scales[:, 4 * q : 4 * q + 4, :].bitcast(I32),
+                planes[32 * q : 32 * q + 4, :].bitcast(I32).rearrange("r (g c) -> r g c", g=PASSES),
+                x_scales[:, 4 * q : 4 * q + 4, :].bitcast(I32).rearrange("g r c -> r g c"),
             )
-        words.append(load_words(1))
         load_weight(0, 0)
+        words.append(load_words(1))
         load_weight(0, 1)
         load_weight(1, 0)
         pos_lists = [load_list("pos1_list", pos1)]
@@ -107,10 +107,10 @@ def tile_picked_zmodd_tanh_po_kernel(
         pos_lists.append(load_list("pos3_list", pos3))
 
         picked = [keep.tile([P, S], U32, name="picked%d" % g, align_bytes=MX_ALIGN) for g in range(PASSES)]
-        picked_scales = keep.tile([P, S], U8, name="picked_scales", align_bytes=MX_ALIGN)
-        nc.vector.tensor_copy(picked[0][:], words[0][:].bitcast(U32).indirect(offs_list[:]))
-        nc.vector.tensor_copy(picked_scales[:], planes[:].indirect(offs_list[:]))
-        nc.vector.tensor_copy(picked[1][:], words[1][:].bitcast(U32).indirect(offs_list[:]))
+        picked_scales = [keep.tile([P, S], U8, name="picked_scales%d" % g, align_bytes=MX_ALIGN) for g in range(PASSES)]
+        for g in range(PASSES):
+            nc.vector.tensor_copy(picked[g][:], words[g][:].bitcast(U32).indirect(offs_list[:]))
+            nc.vector.tensor_copy(picked_scales[g][:], planes[:, g * T : (g + 1) * T].indirect(offs_list[:]))
 
         rounded = {}
         banks = {}
@@ -151,7 +151,7 @@ def tile_picked_zmodd_tanh_po_kernel(
                     lhsT=codes[:, columns].bitcast(FP8X4),
                     lhsT_scale=scales[:, columns],
                     rhs=picked[g][:].bitcast(FP8X4),
-                    rhs_scale=picked_scales[4 * g : P, :],
+                    rhs_scale=picked_scales[g][:],
                     start=(g == 0),
                     stop=(g == PASSES - 1),
                 )
@@ -190,9 +190,9 @@ def tile_picked_zmodd_tanh_po_kernel(
             nc.vector.scalar_tensor_tensor(out, gate, one_half[:], sample, SUBTRACT, MULT)
 
         round_pair(0, 0, 1, P)
-        round_pair(0, 0, 0, 0)
-        multiply_pair(0, 0, 0)
+        round_pair(0, 0, 0, P)
         multiply_pair(0, 0, 1)
+        multiply_pair(0, 0, 0)
         round_pair(0, 1, 1, 0)
         round_pair(0, 1, 0, P)
         for h in PAIRS:

@@ -88,10 +88,10 @@ def tile_picked_zmodd_tanh_po_kernel(
 
         words = [load_words(0)]
         offs_list = load_list("offs_list", offs)
-        for q in range(QUADRANTS):
+        for r in range(4):
             nc.sync.dma_start(
-                planes[32 * q : 32 * q + 4, :].bitcast(I32).rearrange("r (g c) -> r g c", g=PASSES),
-                x_scales[:, 4 * q : 4 * q + 4, :].bitcast(I32).rearrange("g r c -> r g c"),
+                planes[r:P:32, :].bitcast(I32).rearrange("q (g c) -> q g c", g=PASSES),
+                x_scales[:, r:16:4, :].bitcast(I32).rearrange("g q c -> q g c"),
             )
         load_weight(0, 0)
         words.append(load_words(1))

@@ -31,6 +31,7 @@ SETS = (2, 3, 0, 1)
 
 SCALAR_SHARE_W1 = 104
 SCALAR_SHARE_W2 = 80
+GPSIMD_SHARE_SUM = 832
 SCALAR_SHARE_OUT = (48, 32)
 
 
@@ -52,8 +53,9 @@ def tile_picked_zmodd_tanh_po_kernel(
         def of_pair(tile, h):
             return tile[:, 2 * h * V : 2 * (h + 1) * V]
 
-        planes = keep.tile([P, PASSES * T], U8, name="planes", align_bytes=MX_ALIGN)
-        nc.vector.memset(planes[:].bitcast(I32), 0)
+        planes = [keep.tile([P, T], U8, name="plane%d" % g, align_bytes=MX_ALIGN) for g in range(PASSES)]
+        for g in range(PASSES):
+            nc.vector.memset(planes[g][:].bitcast(I32), 0)
 
         zero = keep.tile([P, 1], F32, name="zero")
         nc.vector.memset(zero[:], 0.0)
@@ -79,6 +81,10 @@ def tile_picked_zmodd_tanh_po_kernel(
             nc.sync.dma_start(tile[:], x_words[g].rearrange("p c r -> p (c r)").bitcast(I32))
             return tile
 
+        def load_plane(g):
+            for r in range(4):
+                nc.sync.dma_start(planes[g][4 * g + r : P : 32, :].bitcast(I32), x_scales[g, r:16:4, :].bitcast(I32))
+
         raw = {}
 
         def load_weight(w, g):
@@ -88,13 +94,10 @@ def tile_picked_zmodd_tanh_po_kernel(
 
         words = [load_words(0)]
         offs_list = load_list("offs_list", offs)
-        for r in range(4):
-            nc.sync.dma_start(
-                planes[r:P:32, :].bitcast(I32).rearrange("q (g c) -> q g c", g=PASSES),
-                x_scales[:, r:16:4, :].bitcast(I32).rearrange("g q c -> q g c"),
-            )
+        load_plane(0)
         load_weight(0, 0)
         words.append(load_words(1))
+        load_plane(1)
         load_weight(0, 1)
         load_weight(1, 0)
         pos_lists = [load_list("pos1_list", pos1)]
@@ -110,7 +113,7 @@ def tile_picked_zmodd_tanh_po_kernel(
         picked_scales = [keep.tile([P, S], U8, name="picked_scales%d" % g, align_bytes=MX_ALIGN) for g in range(PASSES)]
         for g in range(PASSES):
             nc.vector.tensor_copy(picked[g][:], words[g][:].bitcast(U32).indirect(offs_list[:]))
-            nc.vector.tensor_copy(picked_scales[g][:], planes[:, g * T : (g + 1) * T].indirect(offs_list[:]))
+            nc.vector.tensor_copy(picked_scales[g][:], planes[g][:].indirect(offs_list[:]))
 
         rounded = {}
         banks = {}
@@ -151,7 +154,7 @@ def tile_picked_zmodd_tanh_po_kernel(
                     lhsT=codes[:, columns].bitcast(FP8X4),
                     lhsT_scale=scales[:, columns],
                     rhs=picked[g][:].bitcast(FP8X4),
-                    rhs_scale=picked_scales[g][:],
+                    rhs_scale=picked_scales[g][4 * g :, :],
                     start=(g == 0),
                     stop=(g == PASSES - 1),
                 )
@@ -186,8 +189,8 @@ def tile_picked_zmodd_tanh_po_kernel(
                 for u in range(2):
                     nc.vector.tensor_copy(of_set(sampled[d, h], u), rows[0, 2 * h + u][:].indirect(pos_lists[d][:]))
 
-        def modulate(out, gate, sample):
-            nc.vector.scalar_tensor_tensor(out, gate, one_half[:], sample, SUBTRACT, MULT)
+        def modulate(out, gate, sample, centre=0.5):
+            nc.vector.scalar_tensor_tensor(out, gate, centre, sample, SUBTRACT, MULT)
 
         round_pair(0, 0, 1, P)
         round_pair(0, 0, 0, P)
@@ -215,7 +218,7 @@ def tile_picked_zmodd_tanh_po_kernel(
 
         pass_on_vector(2, 1)
         terms[0] = float_tile(PACK * V, "terms0", tag=rounded_tag(2, 1, 1))
-        modulate(of_pair(terms[0], 1), gates[0, 1][:], sampled[0, 1][:])
+        modulate(of_pair(terms[0], 1), gates[0, 1][:], sampled[0, 1][:], centre=one_half[:])
         pass_on_vector(3, 0)
         for h in PAIRS:
             gate_pair(1, h)
@@ -229,25 +232,28 @@ def tile_picked_zmodd_tanh_po_kernel(
         for h in PAIRS:
             modulate(of_pair(terms[1], h), gates[1, h][:], sampled[1, h][:])
         partial = keep.tile([P, PACK * V], F32, name="partial")
-        nc.gpsimd.tensor_tensor(partial[:], terms[0][:], terms[1][:], ADD)
+        cut = GPSIMD_SHARE_SUM
+        nc.vector.tensor_tensor(partial[:, cut:], terms[0][:, cut:], terms[1][:, cut:], ADD)
+        nc.gpsimd.tensor_tensor(partial[:, :cut], terms[0][:, :cut], terms[1][:, :cut], ADD)
         sample_tap(2)
 
         for h in PAIRS:
             gate_pair(2, h)
-        terms[2] = float_tile(PACK * V, "terms2")
-        for t in SETS:
-            h, u = divmod(t, 2)
-            modulate(of_set(terms[2], t), of_set(gates[2, h], u), of_set(sampled[2, h], u))
-
         result = keep.tile([P, PACK * V], F32, name="result")
         out_rows = out_0.rearrange("(p t) v -> p (t v)", t=PACK)
 
         def half_of_pair0(tile, a):
             return of_pair(tile, 0).rearrange("p (u v) -> p u v", u=2)[:, :, a * HALF : (a + 1) * HALF]
 
-        for t in (2, 3):
-            nc.vector.tensor_tensor(of_set(result, t), of_set(partial, t), of_set(terms[2], t), ADD)
+        last_terms = [float_tile(V, "last_term%d" % u, tag="last_term%d" % u) for u in range(2)]
+        for u in range(2):
+            modulate(last_terms[u][:], of_set(gates[2, 1], u), of_set(sampled[2, 1], u))
+        for u in range(2):
+            nc.vector.tensor_tensor(of_set(result, 2 + u), of_set(partial, 2 + u), last_terms[u][:], ADD)
         nc.sync.dma_start(of_pair(out_rows, 1), of_pair(result, 1))
+        terms[2] = float_tile(2 * V, "terms2", tag="last_term0")
+        for a in range(2):
+            modulate(half_of_pair0(terms[2], a), half_of_pair0(gates[2, 0], a), half_of_pair0(sampled[2, 0], a))
         for a in range(2):
             nc.vector.tensor_tensor(half_of_pair0(result, a), half_of_pair0(partial, a), half_of_pair0(terms[2], a), ADD)
         nc.sync.dma_start(of_pair(out_rows, 0), of_pair(result, 0))

@@ -31,7 +31,7 @@ SETS = (2, 3, 0, 1)
 
 SCALAR_SHARE_W1 = 104
 SCALAR_SHARE_W2 = 80
-GPSIMD_SHARE_SUM = 832
+GPSIMD_SHARE_SUM = 896
 SCALAR_SHARE_OUT = (48, 32)
 
 
@@ -173,7 +173,7 @@ def tile_picked_zmodd_tanh_po_kernel(
             w = d + 1
             for t in (2 * h, 2 * h + 1):
                 if (w, t) not in rows:
-                    rows[w, t] = float_tile(S, "rows%d%d" % (w, t))
+                    rows[w, t] = float_tile(S, "rows%d%d" % (w, t), tag="rows%d%d" % (w, t))
                 if marks and t == 2 * h:
                     nc.scalar.activation(rows[w, t][:], banks[w, t][:], IDENTITY, bias=marks[0], scale=marks[1])
                 else:
@@ -239,21 +239,20 @@ def tile_picked_zmodd_tanh_po_kernel(
 
         for h in PAIRS:
             gate_pair(2, h)
-        result = keep.tile([P, PACK * V], F32, name="result")
+        terms[2] = float_tile(PACK * V, "terms2")
+        modulate(of_pair(terms[2], 1), gates[2, 1][:], sampled[2, 1][:])
+        for u in range(2):
+            modulate(of_set(terms[2], u), of_set(gates[2, 0], u), of_set(sampled[2, 0], u))
+
+        result = float_tile(PACK * V, "result", tag="rows30")
         out_rows = out_0.rearrange("(p t) v -> p (t v)", t=PACK)
 
         def half_of_pair0(tile, a):
             return of_pair(tile, 0).rearrange("p (u v) -> p u v", u=2)[:, :, a * HALF : (a + 1) * HALF]
 
-        last_terms = [float_tile(V, "last_term%d" % u, tag="last_term%d" % u) for u in range(2)]
-        for u in range(2):
-            modulate(last_terms[u][:], of_set(gates[2, 1], u), of_set(sampled[2, 1], u))
-        for u in range(2):
-            nc.vector.tensor_tensor(of_set(result, 2 + u), of_set(partial, 2 + u), last_terms[u][:], ADD)
+        for t in (2, 3):
+            nc.vector.tensor_tensor(of_set(result, t), of_set(partial, t), of_set(terms[2], t), ADD)
         nc.sync.dma_start(of_pair(out_rows, 1), of_pair(result, 1))
-        terms[2] = float_tile(2 * V, "terms2", tag="last_term0")
-        for a in range(2):
-            modulate(half_of_pair0(terms[2], a), half_of_pair0(gates[2, 0], a), half_of_pair0(sampled[2, 0], a))
         for a in range(2):
             nc.vector.tensor_tensor(half_of_pair0(result, a), half_of_pair0(partial, a), half_of_pair0(terms[2], a), ADD)
         nc.sync.dma_start(of_pair(out_rows, 0), of_pair(result, 0))

@@ -23,13 +23,15 @@ P = 128
 PACK = 4
 PASSES = K // (P * PACK)
 QUADRANTS = 4
+QUADRANT = P // QUADRANTS
+LIVE = 4
 MX_ALIGN = 64
 LINE = 4
 HALF = V // 2
 PAIRS = (1, 0)
 SETS = (2, 3, 0, 1)
 
-SCALAR_SHARE_W1 = 104
+SCALAR_SHARE_W1 = 88
 SCALAR_SHARE_W2 = 80
 GPSIMD_SHARE_SUM = 896
 SCALAR_SHARE_OUT = (48, 32)
@@ -82,8 +84,11 @@ def tile_picked_zmodd_tanh_po_kernel(
             return tile
 
         def load_plane(g):
-            for r in range(4):
-                nc.sync.dma_start(planes[g][4 * g + r : P : 32, :].bitcast(I32), x_scales[g, r:16:4, :].bitcast(I32))
+            for r in range(LIVE):
+                nc.sync.dma_start(
+                    planes[g][LIVE * g + r : P : QUADRANT, :].bitcast(I32),
+                    x_scales[g, r : LIVE * QUADRANTS : LIVE, :].bitcast(I32),
+                )
 
         raw = {}
 
@@ -154,7 +159,7 @@ def tile_picked_zmodd_tanh_po_kernel(
                     lhsT=codes[:, columns].bitcast(FP8X4),
                     lhsT_scale=scales[:, columns],
                     rhs=picked[g][:].bitcast(FP8X4),
-                    rhs_scale=picked_scales[g][4 * g :, :],
+                    rhs_scale=picked_scales[g][LIVE * g :, :],
                     start=(g == 0),
                     stop=(g == PASSES - 1),
                 )
@@ -232,9 +237,9 @@ def tile_picked_zmodd_tanh_po_kernel(
         for h in PAIRS:
             modulate(of_pair(terms[1], h), gates[1, h][:], sampled[1, h][:])
         partial = keep.tile([P, PACK * V], F32, name="partial")
-        cut = GPSIMD_SHARE_SUM
-        nc.vector.tensor_tensor(partial[:, cut:], terms[0][:, cut:], terms[1][:, cut:], ADD)
-        nc.gpsimd.tensor_tensor(partial[:, :cut], terms[0][:, :cut], terms[1][:, :cut], ADD)
+        on_gpsimd, on_vector = slice(0, GPSIMD_SHARE_SUM), slice(GPSIMD_SHARE_SUM, PACK * V)
+        nc.vector.tensor_tensor(partial[:, on_vector], terms[0][:, on_vector], terms[1][:, on_vector], ADD)
+        nc.gpsimd.tensor_tensor(partial[:, on_gpsimd], terms[0][:, on_gpsimd], terms[1][:, on_gpsimd], ADD)
         sample_tap(2)
 
         for h in PAIRS:
@@ -278,6 +283,6 @@ def tile_picked_zmodd_tanh_po_kernel(
         for q in range(QUADRANTS):
             queue = nc.scalar if q % 2 == 0 else nc.sync
             queue.dma_start(
-                out_2[0, 4 * q : 4 * q + 4, :].bitcast(I32),
-                out_scales[32 * q : 32 * q + 4, :].bitcast(I32),
+                out_2[0, LIVE * q : LIVE * (q + 1), :].bitcast(I32),
+                out_scales[QUADRANT * q : QUADRANT * q + LIVE, :].bitcast(I32),
             )

@@ -14,26 +14,23 @@ U8 = mybir.dt.uint8
 FP8X4 = mybir.dt.float8_e4m3fn_x4
 MULT = mybir.AluOpType.mult
 ADD = mybir.AluOpType.add
-SUBTRACT = mybir.AluOpType.subtract
-SIGMOID = mybir.ActivationFunctionType.Sigmoid
+TANH = mybir.ActivationFunctionType.Tanh
 COPY = mybir.ActivationFunctionType.Copy
-IDENTITY = mybir.ActivationFunctionType.Identity
 
 P = 128
 PACK = 4
-PASSES = K // (P * PACK)
+PASSES = 2
 QUADRANTS = 4
-QUADRANT = P // QUADRANTS
+QUADRANT = 32
 LIVE = 4
 MX_ALIGN = 64
 LINE = 4
 HALF = V // 2
 PAIRS = (1, 0)
 SETS = (2, 3, 0, 1)
-
-SCALAR_SHARE_W1 = 88
-SCALAR_SHARE_W2 = 80
-GPSIMD_SHARE_SUM = 896
+UNIT_BYTES = PACK * N * 4
+PLACE_BYTES = UNIT_BYTES // 4
+GPSIMD_SHARE = 672
 SCALAR_SHARE_OUT = (48, 32)
 
 
@@ -44,10 +41,15 @@ def tile_picked_zmodd_tanh_po_kernel(
     weights = [w0, w1, w2, w3]
     with ExitStack() as ctx:
         keep = ctx.enter_context(tc.tile_pool(name="keep", bufs=1))
+        stage = ctx.enter_context(tc.tile_pool(name="stage", bufs=1))
         psum = ctx.enter_context(tc.psum_pool(name="psum", bufs=2))
 
-        def float_tile(columns, name, tag=""):
-            return keep.tile([P, columns], F32, name=name, tag=tag, align_bytes=MX_ALIGN)
+        def float_tile(columns, name, after=None, tag=""):
+            if after is None:
+                return keep.tile([P, columns], F32, name=name, tag=tag, align_bytes=MX_ALIGN)
+            w, g, place = after
+            offset = (PASSES * w + g) * UNIT_BYTES + place * PLACE_BYTES
+            return stage.tile([P, columns], F32, name=name, offset=offset, align_bytes=MX_ALIGN)
 
         def of_set(tile, t):
             return tile[:, t * V : (t + 1) * V]
@@ -55,23 +57,12 @@ def tile_picked_zmodd_tanh_po_kernel(
         def of_pair(tile, h):
             return tile[:, 2 * h * V : 2 * (h + 1) * V]
 
-        planes = [keep.tile([P, T], U8, name="plane%d" % g, align_bytes=MX_ALIGN) for g in range(PASSES)]
-        for g in range(PASSES):
-            nc.vector.memset(planes[g][:].bitcast(I32), 0)
-
+        plane = keep.tile([P, T], U8, name="plane", align_bytes=MX_ALIGN)
+        nc.vector.memset(plane[:].bitcast(I32), 0)
         zero = keep.tile([P, 1], F32, name="zero")
         nc.vector.memset(zero[:], 0.0)
-        one_half = keep.tile([P, 1], F32, name="one_half")
-        nc.scalar.activation(one_half[:], zero[:], SIGMOID)
-
-        rows = {(1, t): float_tile(S, "rows1%d" % t) for t in range(PACK)}
-
-        for t in range(PACK):
-            nc.vector.memset(rows[1, t][:, 0:1], float(t % 2))
-        marks_of_mask0 = [(rows[1, 2 * h][:, 0:1], rows[1, 2 * h + 1][:, 0:1]) for h in range(2)]
-
-        def rounded_tag(w, g, h):
-            return "rounded%d%d%d" % (w, g, h)
+        no_bias = keep.tile([P, 1], F32, name="no_bias")
+        nc.scalar.activation(no_bias[:], zero[:], TANH)
 
         def load_list(name, dram):
             tile = keep.tile(list(dram.shape), U16, name=name)
@@ -83,59 +74,58 @@ def tile_picked_zmodd_tanh_po_kernel(
             nc.sync.dma_start(tile[:], x_words[g].rearrange("p c r -> p (c r)").bitcast(I32))
             return tile
 
-        def load_plane(g):
-            for r in range(LIVE):
-                nc.sync.dma_start(
-                    planes[g][LIVE * g + r : P : QUADRANT, :].bitcast(I32),
-                    x_scales[g, r : LIVE * QUADRANTS : LIVE, :].bitcast(I32),
-                )
-
         raw = {}
 
         def load_weight(w, g):
-            raw[w, g] = keep.tile([P, PACK, N], F32, name="raw%d%d" % (w, g))
+            offset = (PASSES * w + g) * UNIT_BYTES
+            raw[w, g] = stage.tile([P, PACK, N], F32, name="raw%d%d" % (w, g), offset=offset, align_bytes=MX_ALIGN)
             k_rows = weights[w][g * P * PACK : (g + 1) * P * PACK, :]
             nc.sync.dma_start(raw[w, g][:], k_rows.rearrange("(p j) m -> p j m", j=PACK))
 
         words = [load_words(0)]
         offs_list = load_list("offs_list", offs)
-        load_plane(0)
+        for q in range(QUADRANTS):
+            nc.sync.dma_start(
+                plane[QUADRANT * q : QUADRANT * q + PASSES * LIVE, :].bitcast(I32),
+                x_scales[:, LIVE * q : LIVE * (q + 1), :].bitcast(I32),
+            )
         load_weight(0, 0)
         words.append(load_words(1))
-        load_plane(1)
         load_weight(0, 1)
         load_weight(1, 0)
-        pos_lists = [load_list("pos1_list", pos1)]
+        pos_lists = [load_list("pos1_list", pos1), load_list("pos2_list", pos2)]
         load_weight(1, 1)
         cen_list = load_list("cen_list", cen)
         for w in (2, 3):
             for g in range(PASSES):
                 load_weight(w, g)
-        pos_lists.append(load_list("pos2_list", pos2))
         pos_lists.append(load_list("pos3_list", pos3))
 
         picked = [keep.tile([P, S], U32, name="picked%d" % g, align_bytes=MX_ALIGN) for g in range(PASSES)]
-        picked_scales = [keep.tile([P, S], U8, name="picked_scales%d" % g, align_bytes=MX_ALIGN) for g in range(PASSES)]
-        for g in range(PASSES):
+        picked_scales = keep.tile([P, S], U8, name="picked_scales", align_bytes=MX_ALIGN)
+
+        def pick_words(g):
             nc.vector.tensor_copy(picked[g][:], words[g][:].bitcast(U32).indirect(offs_list[:]))
-            nc.vector.tensor_copy(picked_scales[g][:], planes[g][:].indirect(offs_list[:]))
+
+        pick_words(0)
+        nc.vector.tensor_copy(picked_scales[:], plane[:].indirect(offs_list[:]))
 
         rounded = {}
         banks = {}
+        rows = {}
         gates = {}
         sampled = {}
         terms = {}
 
-        def round_pair(w, g, h, scalar_share, marks=None):
+        def rounded_tag(w, g, h):
+            return "rounded%d%d%d" % (w, g, h)
+
+        def round_pair(w, g, h, scalar_share):
             tag = rounded_tag(w, g, h)
             tile = keep.tile([P, 2, P, PACK], BF16, name=tag, tag=tag, align_bytes=MX_ALIGN)
             src = raw[w, g][:].rearrange("p j (i t) -> p i j t", t=PACK)[:, :, :, 2 * h : 2 * h + 2]
             dst = tile[:].rearrange("p u i j -> p i j u")
-            if marks:
-                nc.scalar.activation(
-                    dst[:, :scalar_share], src[:, :scalar_share], IDENTITY, bias=marks[0], scale=marks[1]
-                )
-            elif scalar_share > 0:
+            if scalar_share > 0:
                 nc.scalar.copy(dst[:, :scalar_share], src[:, :scalar_share])
             if scalar_share < P:
                 nc.vector.tensor_copy(dst[:, scalar_share:], src[:, scalar_share:])
@@ -159,104 +149,103 @@ def tile_picked_zmodd_tanh_po_kernel(
                     lhsT=codes[:, columns].bitcast(FP8X4),
                     lhsT_scale=scales[:, columns],
                     rhs=picked[g][:].bitcast(FP8X4),
-                    rhs_scale=picked_scales[g][LIVE * g :, :],
+                    rhs_scale=picked_scales[LIVE * g :, :],
                     start=(g == 0),
                     stop=(g == PASSES - 1),
                 )
 
-        def pass_on_vector(w, g):
-            for h in PAIRS:
-                round_pair(w, g, h, 0)
+        def prepare(w, g, shares=(0, 0)):
+            for h, share in zip(PAIRS, shares):
+                round_pair(w, g, h, share)
             for h in PAIRS:
                 multiply_pair(w, g, h)
 
-        def leave_y(t):
-            rows[0, t] = float_tile(S, "rows0%d" % t)
-            nc.scalar.activation(rows[0, t][:], banks[0, t][:], COPY, scale=2.0)
+        def leave(w, t, engine="scalar"):
+            rows[w, t] = float_tile(S, "rows%d%d" % (w, t))
+            if engine == "vector":
+                nc.vector.tensor_copy(rows[w, t][:], banks[w, t][:])
+            elif w == 0:
+                nc.scalar.copy(rows[w, t][:], banks[w, t][:])
+            else:
+                nc.scalar.activation(rows[w, t][:], banks[w, t][:], TANH, bias=no_bias[:])
 
-        def gate_pair(d, h, marks=None):
-            w = d + 1
+        def gather(out, window, engine):
+            if engine == "scalar":
+                nc.scalar.activation(out, window, COPY)
+            else:
+                nc.vector.tensor_copy(out, window)
+
+        def gate_pair(d, h, engine="scalar"):
+            if d not in gates:
+                gates[d] = float_tile(PACK * V, "gates%d" % d)
             for t in (2 * h, 2 * h + 1):
-                if (w, t) not in rows:
-                    rows[w, t] = float_tile(S, "rows%d%d" % (w, t), tag="rows%d%d" % (w, t))
-                if marks and t == 2 * h:
-                    nc.scalar.activation(rows[w, t][:], banks[w, t][:], IDENTITY, bias=marks[0], scale=marks[1])
-                else:
-                    nc.scalar.copy(rows[w, t][:], banks[w, t][:])
-            gates[d, h] = float_tile(2 * V, "gates%d%d" % (d, h))
-            for u in range(2):
-                gathered_sums = rows[w, 2 * h + u][:].indirect(cen_list[:])
-                nc.scalar.activation(of_set(gates[d, h], u), gathered_sums, SIGMOID, scale=2.0)
+                leave(d + 1, t)
+            for t in (2 * h, 2 * h + 1):
+                gather(of_set(gates[d], t), rows[d + 1, t][:].indirect(cen_list[:]), engine)
 
-        def sample_tap(d):
-            for h in PAIRS:
-                sampled[d, h] = float_tile(2 * V, "sampled%d%d" % (d, h))
-                for u in range(2):
-                    nc.vector.tensor_copy(of_set(sampled[d, h], u), rows[0, 2 * h + u][:].indirect(pos_lists[d][:]))
+        def sample(d, sets, engine, after=None):
+            tile = float_tile(len(sets) * V, "sampled%d%d" % (d, sets[0]), after)
+            sampled[d, sets] = tile
+            for u, t in enumerate(sets):
+                gather(of_set(tile, u), rows[0, t][:].indirect(pos_lists[d][:]), engine)
 
-        def modulate(out, gate, sample, centre=0.5):
-            nc.vector.scalar_tensor_tensor(out, gate, centre, sample, SUBTRACT, MULT)
+        def modulate(engine, d, sets):
+            columns = slice(sets[0] * V, (sets[-1] + 1) * V)
+            engine.tensor_tensor(terms[d][:, columns], gates[d][:, columns], sampled[d, sets][:], MULT)
 
-        round_pair(0, 0, 1, P)
+        round_pair(0, 0, 1, 0)
         round_pair(0, 0, 0, P)
         multiply_pair(0, 0, 1)
+        pick_words(1)
         multiply_pair(0, 0, 0)
-        round_pair(0, 1, 1, 0)
-        round_pair(0, 1, 0, P)
-        for h in PAIRS:
-            multiply_pair(0, 1, h)
+        prepare(0, 1, (44, 44))
+        leave(0, 2, "vector")
+        for t in SETS[1:]:
+            leave(0, t)
+        prepare(1, 0)
+        sampled[0] = float_tile(PACK * V, "sampled0")
         for t in SETS:
-            leave_y(t)
-
-        pass_on_vector(1, 0)
-        sample_tap(0)
-        round_pair(1, 1, 1, P)
-        round_pair(1, 1, 0, SCALAR_SHARE_W1)
+            gather(of_set(sampled[0], t), rows[0, t][:].indirect(pos_lists[0][:]), "scalar")
+        sample(1, (2,), "scalar")
+        prepare(1, 1)
+        sample(1, (3,), "vector", (1, 1, 0))
+        prepare(2, 0)
         for h in PAIRS:
-            multiply_pair(1, 1, h)
-        round_pair(2, 0, 1, 0)
-        round_pair(2, 0, 0, SCALAR_SHARE_W2, marks=marks_of_mask0[1])
-        for h in PAIRS:
-            multiply_pair(2, 0, h)
-        gate_pair(0, 1, marks=marks_of_mask0[0])
-        gate_pair(0, 0)
-
-        pass_on_vector(2, 1)
-        terms[0] = float_tile(PACK * V, "terms0", tag=rounded_tag(2, 1, 1))
-        modulate(of_pair(terms[0], 1), gates[0, 1][:], sampled[0, 1][:], centre=one_half[:])
-        pass_on_vector(3, 0)
+            gate_pair(0, h)
+        prepare(2, 1)
+        on_gpsimd, on_vector = slice(0, GPSIMD_SHARE), slice(GPSIMD_SHARE, PACK * V)
+        first_terms = float_tile(PACK * V - GPSIMD_SHARE, "first_terms", (2, 1, 0))
+        nc.vector.tensor_tensor(first_terms[:], gates[0][:, on_vector], sampled[0][:, on_vector], MULT)
+        prepare(3, 0)
         for h in PAIRS:
             gate_pair(1, h)
-        pass_on_vector(3, 1)
-
-        centred = float_tile(2 * V, "centred", tag=rounded_tag(3, 1, 1))
-        nc.gpsimd.tensor_scalar(centred[:], gates[0, 0][:], 1.0, -0.5, MULT, ADD)
-        nc.gpsimd.tensor_tensor(of_pair(terms[0], 0), centred[:], sampled[0, 0][:], MULT)
-        sample_tap(1)
-        terms[1] = float_tile(PACK * V, "terms1")
-        for h in PAIRS:
-            modulate(of_pair(terms[1], h), gates[1, h][:], sampled[1, h][:])
+        prepare(3, 1)
+        terms[0] = float_tile(GPSIMD_SHARE, "terms0", tag=rounded_tag(3, 1, 1))
+        nc.gpsimd.tensor_tensor(terms[0][:], gates[0][:, on_gpsimd], sampled[0][:, on_gpsimd], MULT)
+        sample(1, (0, 1), "vector", (3, 1, 0))
+        sample(2, (2,), "vector", (3, 1, 1))
+        terms[1] = float_tile(PACK * V, "terms1", (3, 1, 2))
+        for sets in ((2,), (3,), (0, 1)):
+            modulate(nc.vector, 1, sets)
         partial = keep.tile([P, PACK * V], F32, name="partial")
-        on_gpsimd, on_vector = slice(0, GPSIMD_SHARE_SUM), slice(GPSIMD_SHARE_SUM, PACK * V)
-        nc.vector.tensor_tensor(partial[:, on_vector], terms[0][:, on_vector], terms[1][:, on_vector], ADD)
-        nc.gpsimd.tensor_tensor(partial[:, on_gpsimd], terms[0][:, on_gpsimd], terms[1][:, on_gpsimd], ADD)
-        sample_tap(2)
-
+        nc.vector.tensor_tensor(partial[:, on_vector], first_terms[:], terms[1][:, on_vector], ADD)
+        nc.gpsimd.tensor_tensor(partial[:, on_gpsimd], terms[0][:], terms[1][:, on_gpsimd], ADD)
+        sample(2, (3,), "vector", (3, 0, 0))
+        sample(2, (0, 1), "vector", (3, 0, 1))
         for h in PAIRS:
             gate_pair(2, h)
         terms[2] = float_tile(PACK * V, "terms2")
-        modulate(of_pair(terms[2], 1), gates[2, 1][:], sampled[2, 1][:])
-        for u in range(2):
-            modulate(of_set(terms[2], u), of_set(gates[2, 0], u), of_set(sampled[2, 0], u))
-
+        for t in (2, 3):
+            modulate(nc.vector, 2, (t,))
         result = float_tile(PACK * V, "result", tag="rows30")
         out_rows = out_0.rearrange("(p t) v -> p (t v)", t=PACK)
 
         def half_of_pair0(tile, a):
             return of_pair(tile, 0).rearrange("p (u v) -> p u v", u=2)[:, :, a * HALF : (a + 1) * HALF]
 
-        for t in (2, 3):
-            nc.vector.tensor_tensor(of_set(result, t), of_set(partial, t), of_set(terms[2], t), ADD)
+        for t in range(2):
+            nc.vector.tensor_tensor(of_set(terms[2], t), of_set(gates[2], t), of_set(sampled[2, (0, 1)], t), MULT)
+            nc.vector.tensor_tensor(of_set(result, t + 2), of_set(partial, t + 2), of_set(terms[2], t + 2), ADD)
         nc.sync.dma_start(of_pair(out_rows, 1), of_pair(result, 1))
         for a in range(2):
             nc.vector.tensor_tensor(half_of_pair0(result, a), half_of_pair0(partial, a), half_of_pair0(terms[2], a), ADD)

@@ -14,7 +14,8 @@ U8 = mybir.dt.uint8
 FP8X4 = mybir.dt.float8_e4m3fn_x4
 MULT = mybir.AluOpType.mult
 ADD = mybir.AluOpType.add
-TANH = mybir.ActivationFunctionType.Tanh
+SUBTRACT = mybir.AluOpType.subtract
+SIGMOID = mybir.ActivationFunctionType.Sigmoid
 COPY = mybir.ActivationFunctionType.Copy
 
 P = 128
@@ -30,7 +31,8 @@ PAIRS = (1, 0)
 SETS = (2, 3, 0, 1)
 UNIT_BYTES = PACK * N * 4
 PLACE_BYTES = UNIT_BYTES // 4
-GPSIMD_SHARE = 672
+GPSIMD_SHARE_TERM = 512
+GPSIMD_SHARE_SUM = 512
 SCALAR_SHARE_OUT = (48, 32)
 
 
@@ -61,8 +63,8 @@ def tile_picked_zmodd_tanh_po_kernel(
         nc.vector.memset(plane[:].bitcast(I32), 0)
         zero = keep.tile([P, 1], F32, name="zero")
         nc.vector.memset(zero[:], 0.0)
-        no_bias = keep.tile([P, 1], F32, name="no_bias")
-        nc.scalar.activation(no_bias[:], zero[:], TANH)
+        one_half = keep.tile([P, 1], F32, name="one_half")
+        nc.scalar.activation(one_half[:], zero[:], SIGMOID)
 
         def load_list(name, dram):
             tile = keep.tile(list(dram.shape), U16, name=name)
@@ -163,11 +165,11 @@ def tile_picked_zmodd_tanh_po_kernel(
         def leave(w, t, engine="scalar"):
             rows[w, t] = float_tile(S, "rows%d%d" % (w, t))
             if engine == "vector":
-                nc.vector.tensor_copy(rows[w, t][:], banks[w, t][:])
+                nc.vector.tensor_scalar(rows[w, t][:], banks[w, t][:], 2.0, None, MULT)
             elif w == 0:
-                nc.scalar.copy(rows[w, t][:], banks[w, t][:])
+                nc.scalar.activation(rows[w, t][:], banks[w, t][:], COPY, scale=2.0)
             else:
-                nc.scalar.activation(rows[w, t][:], banks[w, t][:], TANH, bias=no_bias[:])
+                nc.scalar.copy(rows[w, t][:], banks[w, t][:])
 
         def gather(out, window, engine):
             if engine == "scalar":
@@ -175,13 +177,13 @@ def tile_picked_zmodd_tanh_po_kernel(
             else:
                 nc.vector.tensor_copy(out, window)
 
-        def gate_pair(d, h, engine="scalar"):
+        def gate_pair(d, h):
             if d not in gates:
                 gates[d] = float_tile(PACK * V, "gates%d" % d)
             for t in (2 * h, 2 * h + 1):
                 leave(d + 1, t)
             for t in (2 * h, 2 * h + 1):
-                gather(of_set(gates[d], t), rows[d + 1, t][:].indirect(cen_list[:]), engine)
+                nc.scalar.activation(of_set(gates[d], t), rows[d + 1, t][:].indirect(cen_list[:]), SIGMOID, scale=2.0)
 
         def sample(d, sets, engine, after=None):
             tile = float_tile(len(sets) * V, "sampled%d%d" % (d, sets[0]), after)
@@ -189,9 +191,12 @@ def tile_picked_zmodd_tanh_po_kernel(
             for u, t in enumerate(sets):
                 gather(of_set(tile, u), rows[0, t][:].indirect(pos_lists[d][:]), engine)
 
-        def modulate(engine, d, sets):
+        def modulate(out, gate, sample, centre=0.5):
+            nc.vector.scalar_tensor_tensor(out, gate, centre, sample, SUBTRACT, MULT)
+
+        def modulate_sets(d, sets):
             columns = slice(sets[0] * V, (sets[-1] + 1) * V)
-            engine.tensor_tensor(terms[d][:, columns], gates[d][:, columns], sampled[d, sets][:], MULT)
+            modulate(terms[d][:, columns], gates[d][:, columns], sampled[d, sets][:])
 
         round_pair(0, 0, 1, 0)
         round_pair(0, 0, 0, P)
@@ -199,44 +204,41 @@ def tile_picked_zmodd_tanh_po_kernel(
         pick_words(1)
         multiply_pair(0, 0, 0)
         prepare(0, 1, (44, 44))
-        leave(0, 2, "vector")
-        for t in SETS[1:]:
+        for t in SETS:
             leave(0, t)
         prepare(1, 0)
         sampled[0] = float_tile(PACK * V, "sampled0")
         for t in SETS:
             gather(of_set(sampled[0], t), rows[0, t][:].indirect(pos_lists[0][:]), "scalar")
-        sample(1, (2,), "scalar")
+        sample(1, (2,), "vector", (1, 0, 0))
         prepare(1, 1)
-        sample(1, (3,), "vector", (1, 1, 0))
         prepare(2, 0)
+        sample(1, (3,), "vector", (2, 0, 0))
         for h in PAIRS:
             gate_pair(0, h)
         prepare(2, 1)
-        on_gpsimd, on_vector = slice(0, GPSIMD_SHARE), slice(GPSIMD_SHARE, PACK * V)
-        first_terms = float_tile(PACK * V - GPSIMD_SHARE, "first_terms", (2, 1, 0))
-        nc.vector.tensor_tensor(first_terms[:], gates[0][:, on_vector], sampled[0][:, on_vector], MULT)
+        terms[0] = float_tile(PACK * V, "terms0", (2, 1, 0))
+        modulate(of_pair(terms[0], 1), of_pair(gates[0], 1), of_pair(sampled[0], 1), centre=one_half[:])
         prepare(3, 0)
+        modulate(of_pair(terms[0], 0), of_pair(gates[0], 0), of_pair(sampled[0], 0))
         for h in PAIRS:
             gate_pair(1, h)
         prepare(3, 1)
-        terms[0] = float_tile(GPSIMD_SHARE, "terms0", tag=rounded_tag(3, 1, 1))
-        nc.gpsimd.tensor_tensor(terms[0][:], gates[0][:, on_gpsimd], sampled[0][:, on_gpsimd], MULT)
         sample(1, (0, 1), "vector", (3, 1, 0))
-        sample(2, (2,), "vector", (3, 1, 1))
         terms[1] = float_tile(PACK * V, "terms1", (3, 1, 2))
-        for sets in ((2,), (3,), (0, 1)):
-            modulate(nc.vector, 1, sets)
+        for sets in ((2,), (3,)):
+            modulate_sets(1, sets)
+        modulate_sets(1, (0, 1))
         partial = keep.tile([P, PACK * V], F32, name="partial")
-        nc.vector.tensor_tensor(partial[:, on_vector], first_terms[:], terms[1][:, on_vector], ADD)
-        nc.gpsimd.tensor_tensor(partial[:, on_gpsimd], terms[0][:], terms[1][:, on_gpsimd], ADD)
-        sample(2, (3,), "vector", (3, 0, 0))
+        on_gpsimd, on_vector = slice(0, 896), slice(896, PACK * V)
+        nc.vector.tensor_tensor(partial[:, on_vector], terms[0][:, on_vector], terms[1][:, on_vector], ADD)
+        nc.gpsimd.tensor_tensor(partial[:, on_gpsimd], terms[0][:, on_gpsimd], terms[1][:, on_gpsimd], ADD)
+        sample(2, (2, 3), "vector", (3, 0, 0))
         sample(2, (0, 1), "vector", (3, 0, 1))
         for h in PAIRS:
             gate_pair(2, h)
         terms[2] = float_tile(PACK * V, "terms2")
-        for t in (2, 3):
-            modulate(nc.vector, 2, (t,))
+        modulate_sets(2, (2, 3))
         result = float_tile(PACK * V, "result", tag="rows30")
         out_rows = out_0.rearrange("(p t) v -> p (t v)", t=PACK)
 
@@ -244,7 +246,7 @@ def tile_picked_zmodd_tanh_po_kernel(
             return of_pair(tile, 0).rearrange("p (u v) -> p u v", u=2)[:, :, a * HALF : (a + 1) * HALF]
 
         for t in range(2):
-            nc.vector.tensor_tensor(of_set(terms[2], t), of_set(gates[2], t), of_set(sampled[2, (0, 1)], t), MULT)
+            modulate(of_set(terms[2], t), of_set(gates[2], t), of_set(sampled[2, (0, 1)], t))
             nc.vector.tensor_tensor(of_set(result, t + 2), of_set(partial, t + 2), of_set(terms[2], t + 2), ADD)
         nc.sync.dma_start(of_pair(out_rows, 1), of_pair(result, 1))
         for a in range(2):

@@ -31,8 +31,9 @@ PAIRS = (1, 0)
 SETS = (2, 3, 0, 1)
 UNIT_BYTES = PACK * N * 4
 PLACE_BYTES = UNIT_BYTES // 4
-GPSIMD_SHARE_TERM = 512
-GPSIMD_SHARE_SUM = 512
+HALF_LIST = S // 2
+GPSIMD_SHARE_SUM = 896
+SCALAR_SHARE_FIRST = 32
 SCALAR_SHARE_OUT = (48, 32)
 
 
@@ -92,8 +93,8 @@ def tile_picked_zmodd_tanh_po_kernel(
                 x_scales[:, LIVE * q : LIVE * (q + 1), :].bitcast(I32),
             )
         load_weight(0, 0)
-        words.append(load_words(1))
         load_weight(0, 1)
+        words.append(load_words(1))
         load_weight(1, 0)
         pos_lists = [load_list("pos1_list", pos1), load_list("pos2_list", pos2)]
         load_weight(1, 1)
@@ -106,10 +107,12 @@ def tile_picked_zmodd_tanh_po_kernel(
         picked = [keep.tile([P, S], U32, name="picked%d" % g, align_bytes=MX_ALIGN) for g in range(PASSES)]
         picked_scales = keep.tile([P, S], U8, name="picked_scales", align_bytes=MX_ALIGN)
 
-        def pick_words(g):
-            nc.vector.tensor_copy(picked[g][:], words[g][:].bitcast(U32).indirect(offs_list[:]))
+        def pick_words(g, entries):
+            offsets = offs_list[:, entries.start // 16 : entries.stop // 16]
+            nc.vector.tensor_copy(picked[g][:, entries], words[g][:].bitcast(U32).indirect(offsets))
 
-        pick_words(0)
+        list_halves = [slice(a * HALF_LIST, (a + 1) * HALF_LIST) for a in range(2)]
+        pick_words(0, slice(0, S))
         nc.vector.tensor_copy(picked_scales[:], plane[:].indirect(offs_list[:]))
 
         rounded = {}
@@ -133,7 +136,9 @@ def tile_picked_zmodd_tanh_po_kernel(
                 nc.vector.tensor_copy(dst[:, scalar_share:], src[:, scalar_share:])
             rounded[w, g, h] = tile
 
-        def multiply_pair(w, g, h):
+        quantised = {}
+
+        def quantise_pair(w, g, h):
             codes = keep.tile([P, 2 * P], U32, name="codes%d%d%d" % (w, g, h), align_bytes=MX_ALIGN)
             scales = keep.tile([P, 2 * P], U8, name="scales%d%d%d" % (w, g, h), align_bytes=MX_ALIGN)
             nc.vector.quantize_mx(
@@ -141,35 +146,35 @@ def tile_picked_zmodd_tanh_po_kernel(
                 scales=scales[:],
                 in_=rounded[w, g, h][:].rearrange("p u i j -> p (u i j)"),
             )
+            quantised[w, g, h] = (codes, scales)
+
+        def multiply_pair(w, g, h, entries):
+            codes, scales = quantised[w, g, h]
             for u in range(2):
                 t = 2 * h + u
                 if g == 0:
-                    banks[w, t] = psum.tile([P, S], F32, name="bank%d" % t)
+                    banks[w, t, entries.start] = psum.tile([P, S], F32, name="bank%d" % t)
                 columns = slice(u * P, (u + 1) * P)
                 nc.tensor.matmul_mx(
-                    out=banks[w, t][:],
+                    out=banks[w, t, entries.start][:, entries],
                     lhsT=codes[:, columns].bitcast(FP8X4),
                     lhsT_scale=scales[:, columns],
-                    rhs=picked[g][:].bitcast(FP8X4),
-                    rhs_scale=picked_scales[LIVE * g :, :],
+                    rhs=picked[g][:, entries].bitcast(FP8X4),
+                    rhs_scale=picked_scales[LIVE * g :, entries],
                     start=(g == 0),
                     stop=(g == PASSES - 1),
                 )
 
-        def prepare(w, g, shares=(0, 0)):
-            for h, share in zip(PAIRS, shares):
-                round_pair(w, g, h, share)
+        def prepare(w, g):
             for h in PAIRS:
-                multiply_pair(w, g, h)
+                round_pair(w, g, h, 0)
+            for h in PAIRS:
+                quantise_pair(w, g, h)
+                multiply_pair(w, g, h, slice(0, S))
 
-        def leave(w, t, engine="scalar"):
+        def leave(w, t):
             rows[w, t] = float_tile(S, "rows%d%d" % (w, t))
-            if engine == "vector":
-                nc.vector.tensor_scalar(rows[w, t][:], banks[w, t][:], 2.0, None, MULT)
-            elif w == 0:
-                nc.scalar.activation(rows[w, t][:], banks[w, t][:], COPY, scale=2.0)
-            else:
-                nc.scalar.copy(rows[w, t][:], banks[w, t][:])
+            nc.scalar.copy(rows[w, t][:], banks[w, t, 0][:])
 
         def gather(out, window, engine):
             if engine == "scalar":
@@ -198,18 +203,31 @@ def tile_picked_zmodd_tanh_po_kernel(
             columns = slice(sets[0] * V, (sets[-1] + 1) * V)
             modulate(terms[d][:, columns], gates[d][:, columns], sampled[d, sets][:])
 
+        first_pieces = {1: list_halves, 0: [slice(0, S)]}
         round_pair(0, 0, 1, 0)
         round_pair(0, 0, 0, P)
-        multiply_pair(0, 0, 1)
-        pick_words(1)
-        multiply_pair(0, 0, 0)
-        prepare(0, 1, (44, 44))
-        for t in SETS:
-            leave(0, t)
+        for h in PAIRS:
+            quantise_pair(0, 0, h)
+            for entries in first_pieces[h]:
+                multiply_pair(0, 0, h, entries)
+        round_pair(0, 1, 1, SCALAR_SHARE_FIRST)
+        round_pair(0, 1, 0, P)
+        quantise_pair(0, 1, 1)
+        for entries in list_halves:
+            pick_words(1, entries)
+        quantise_pair(0, 1, 0)
+        for h in PAIRS:
+            for t in (2 * h, 2 * h + 1):
+                rows[0, t] = float_tile(S, "rows0%d" % t)
+            for entries in first_pieces[h]:
+                multiply_pair(0, 1, h, entries)
+                for t in (2 * h, 2 * h + 1):
+                    nc.scalar.activation(rows[0, t][:, entries], banks[0, t, entries.start][:, entries], COPY, scale=2.0)
         prepare(1, 0)
         sampled[0] = float_tile(PACK * V, "sampled0")
         for t in SETS:
             gather(of_set(sampled[0], t), rows[0, t][:].indirect(pos_lists[0][:]), "scalar")
+        sample(1, (0,), "scalar")
         sample(1, (2,), "vector", (1, 0, 0))
         prepare(1, 1)
         prepare(2, 0)
@@ -224,33 +242,44 @@ def tile_picked_zmodd_tanh_po_kernel(
         for h in PAIRS:
             gate_pair(1, h)
         prepare(3, 1)
-        sample(1, (0, 1), "vector", (3, 1, 0))
+        sample(1, (1,), "vector", (3, 1, 0))
         terms[1] = float_tile(PACK * V, "terms1", (3, 1, 2))
-        for sets in ((2,), (3,)):
-            modulate_sets(1, sets)
-        modulate_sets(1, (0, 1))
+        for t in SETS:
+            modulate_sets(1, (t,))
         partial = keep.tile([P, PACK * V], F32, name="partial")
-        on_gpsimd, on_vector = slice(0, 896), slice(896, PACK * V)
+        on_gpsimd, on_vector = slice(0, GPSIMD_SHARE_SUM), slice(GPSIMD_SHARE_SUM, PACK * V)
         nc.vector.tensor_tensor(partial[:, on_vector], terms[0][:, on_vector], terms[1][:, on_vector], ADD)
         nc.gpsimd.tensor_tensor(partial[:, on_gpsimd], terms[0][:, on_gpsimd], terms[1][:, on_gpsimd], ADD)
         sample(2, (2, 3), "vector", (3, 0, 0))
         sample(2, (0, 1), "vector", (3, 0, 1))
         for h in PAIRS:
             gate_pair(2, h)
-        terms[2] = float_tile(PACK * V, "terms2")
-        modulate_sets(2, (2, 3))
-        result = float_tile(PACK * V, "result", tag="rows30")
+        result = float_tile(PACK * V, "result")
         out_rows = out_0.rearrange("(p t) v -> p (t v)", t=PACK)
+        last = {}
 
-        def half_of_pair0(tile, a):
-            return of_pair(tile, 0).rearrange("p (u v) -> p u v", u=2)[:, :, a * HALF : (a + 1) * HALF]
+        def modulate_last(t, columns):
+            if t not in last:
+                last[t] = float_tile(V, "last%d" % t, tag="last%d" % (t % 2))
+            sets = (2 * (t // 2), 2 * (t // 2) + 1)
+            modulate(last[t][:, columns], of_set(gates[2], t)[:, columns], of_set(sampled[2, sets], t % 2)[:, columns])
 
-        for t in range(2):
-            modulate(of_set(terms[2], t), of_set(gates[2], t), of_set(sampled[2, (0, 1)], t))
-            nc.vector.tensor_tensor(of_set(result, t + 2), of_set(partial, t + 2), of_set(terms[2], t + 2), ADD)
+        def add_last(t, columns):
+            nc.vector.tensor_tensor(of_set(result, t)[:, columns], of_set(partial, t)[:, columns], last[t][:, columns], ADD)
+
+        whole = slice(0, V)
+        halves = [slice(a * HALF, (a + 1) * HALF) for a in range(2)]
+        for t in (2, 3):
+            modulate_last(t, whole)
+        for t in (2, 3):
+            add_last(t, whole)
         nc.sync.dma_start(of_pair(out_rows, 1), of_pair(result, 1))
-        for a in range(2):
-            nc.vector.tensor_tensor(half_of_pair0(result, a), half_of_pair0(partial, a), half_of_pair0(terms[2], a), ADD)
+        modulate_last(0, whole)
+        for columns in halves:
+            modulate_last(1, columns)
+        add_last(0, whole)
+        for columns in halves:
+            add_last(1, columns)
         nc.sync.dma_start(of_pair(out_rows, 0), of_pair(result, 0))
 
         out_rounded = keep.tile([P, V * PACK], BF16, name="out_rounded", align_bytes=MX_ALIGN)

@@ -34,6 +34,7 @@ PLACE_BYTES = UNIT_BYTES // 4
 HALF_LIST = S // 2
 GPSIMD_SHARE_SUM = 896
 SCALAR_SHARE_FIRST = 32
+SCALAR_SHARE_TAP1 = 160
 SCALAR_SHARE_OUT = (48, 32)
 
 
@@ -188,7 +189,10 @@ def tile_picked_zmodd_tanh_po_kernel(
             for t in (2 * h, 2 * h + 1):
                 leave(d + 1, t)
             for t in (2 * h, 2 * h + 1):
-                nc.scalar.activation(of_set(gates[d], t), rows[d + 1, t][:].indirect(cen_list[:]), SIGMOID, scale=2.0)
+                width = HALF if (d, t) == (2, 1) else V
+                for first in range(0, V, width):
+                    sums = rows[d + 1, t][:].indirect(cen_list[:, first // 16 : (first + width) // 16])
+                    nc.scalar.activation(of_set(gates[d], t)[:, first : first + width], sums, SIGMOID, scale=2.0)
 
         def sample(d, sets, engine, after=None):
             tile = float_tile(len(sets) * V, "sampled%d%d" % (d, sets[0]), after)
@@ -227,7 +231,8 @@ def tile_picked_zmodd_tanh_po_kernel(
         sampled[0] = float_tile(PACK * V, "sampled0")
         for t in SETS:
             gather(of_set(sampled[0], t), rows[0, t][:].indirect(pos_lists[0][:]), "scalar")
-        sample(1, (0,), "scalar")
+        early_part = float_tile(SCALAR_SHARE_TAP1, "early_part")
+        gather(early_part[:], rows[0, 0][:].indirect(pos_lists[1][:, : SCALAR_SHARE_TAP1 // 16]), "scalar")
         sample(1, (2,), "vector", (1, 0, 0))
         prepare(1, 1)
         prepare(2, 0)
@@ -242,10 +247,15 @@ def tile_picked_zmodd_tanh_po_kernel(
         for h in PAIRS:
             gate_pair(1, h)
         prepare(3, 1)
-        sample(1, (1,), "vector", (3, 1, 0))
+        rest = V - SCALAR_SHARE_TAP1
+        late_part = float_tile(rest + V, "late_part", (3, 1, 0))
+        gather(late_part[:, :rest], rows[0, 0][:].indirect(pos_lists[1][:, SCALAR_SHARE_TAP1 // 16 :]), "vector")
+        gather(late_part[:, rest:], rows[0, 1][:].indirect(pos_lists[1][:]), "vector")
         terms[1] = float_tile(PACK * V, "terms1", (3, 1, 2))
-        for t in SETS:
+        for t in (2, 3):
             modulate_sets(1, (t,))
+        for part, columns in ((early_part, slice(0, SCALAR_SHARE_TAP1)), (late_part, slice(SCALAR_SHARE_TAP1, 2 * V))):
+            modulate(terms[1][:, columns], gates[1][:, columns], part[:])
         partial = keep.tile([P, PACK * V], F32, name="partial")
         on_gpsimd, on_vector = slice(0, GPSIMD_SHARE_SUM), slice(GPSIMD_SHARE_SUM, PACK * V)
         nc.vector.tensor_tensor(partial[:, on_vector], terms[0][:, on_vector], terms[1][:, on_vector], ADD)

@@ -32,9 +32,7 @@ SETS = (2, 3, 0, 1)
 UNIT_BYTES = PACK * N * 4
 PLACE_BYTES = UNIT_BYTES // 4
 HALF_LIST = S // 2
-GPSIMD_SHARE_SUM = 896
 SCALAR_SHARE_FIRST = 32
-SCALAR_SHARE_TAP1 = 160
 SCALAR_SHARE_OUT = (48, 32)
 
 
@@ -121,7 +119,6 @@ def tile_picked_zmodd_tanh_po_kernel(
         rows = {}
         gates = {}
         sampled = {}
-        terms = {}
 
         def rounded_tag(w, g, h):
             return "rounded%d%d%d" % (w, g, h)
@@ -175,7 +172,10 @@ def tile_picked_zmodd_tanh_po_kernel(
 
         def leave(w, t):
             rows[w, t] = float_tile(S, "rows%d%d" % (w, t))
-            nc.scalar.copy(rows[w, t][:], banks[w, t, 0][:])
+            if (w, t) == (1, SETS[0]):
+                nc.scalar.activation(rows[w, t][:], banks[w, t, 0][:], COPY, scale=4.0)
+            else:
+                nc.scalar.copy(rows[w, t][:], banks[w, t, 0][:])
 
         def gather(out, window, engine):
             if engine == "scalar":
@@ -190,9 +190,10 @@ def tile_picked_zmodd_tanh_po_kernel(
                 leave(d + 1, t)
             for t in (2 * h, 2 * h + 1):
                 width = HALF if (d, t) == (2, 1) else V
+                scale = one_half[:] if (d, t) == (0, SETS[0]) else 2.0
                 for first in range(0, V, width):
                     sums = rows[d + 1, t][:].indirect(cen_list[:, first // 16 : (first + width) // 16])
-                    nc.scalar.activation(of_set(gates[d], t)[:, first : first + width], sums, SIGMOID, scale=2.0)
+                    nc.scalar.activation(of_set(gates[d], t)[:, first : first + width], sums, SIGMOID, scale=scale)
 
         def sample(d, sets, engine, after=None):
             tile = float_tile(len(sets) * V, "sampled%d%d" % (d, sets[0]), after)
@@ -200,12 +201,8 @@ def tile_picked_zmodd_tanh_po_kernel(
             for u, t in enumerate(sets):
                 gather(of_set(tile, u), rows[0, t][:].indirect(pos_lists[d][:]), engine)
 
-        def modulate(out, gate, sample, centre=0.5):
-            nc.vector.scalar_tensor_tensor(out, gate, centre, sample, SUBTRACT, MULT)
-
-        def modulate_sets(d, sets):
-            columns = slice(sets[0] * V, (sets[-1] + 1) * V)
-            modulate(terms[d][:, columns], gates[d][:, columns], sampled[d, sets][:])
+        def modulate(out, gate, sample):
+            nc.vector.scalar_tensor_tensor(out, gate, 0.5, sample, SUBTRACT, MULT)
 
         first_pieces = {1: list_halves, 0: [slice(0, S)]}
         round_pair(0, 0, 1, 0)
@@ -231,8 +228,7 @@ def tile_picked_zmodd_tanh_po_kernel(
         sampled[0] = float_tile(PACK * V, "sampled0")
         for t in SETS:
             gather(of_set(sampled[0], t), rows[0, t][:].indirect(pos_lists[0][:]), "scalar")
-        early_part = float_tile(SCALAR_SHARE_TAP1, "early_part")
-        gather(early_part[:], rows[0, 0][:].indirect(pos_lists[1][:, : SCALAR_SHARE_TAP1 // 16]), "scalar")
+        sample(1, (0,), "scalar")
         sample(1, (2,), "vector", (1, 0, 0))
         prepare(1, 1)
         prepare(2, 0)
@@ -240,28 +236,27 @@ def tile_picked_zmodd_tanh_po_kernel(
         for h in PAIRS:
             gate_pair(0, h)
         prepare(2, 1)
-        terms[0] = float_tile(PACK * V, "terms0", (2, 1, 0))
-        modulate(of_pair(terms[0], 1), of_pair(gates[0], 1), of_pair(sampled[0], 1), centre=one_half[:])
+        sample(1, (1,), "vector", (2, 1, 0))
         prepare(3, 0)
-        modulate(of_pair(terms[0], 0), of_pair(gates[0], 0), of_pair(sampled[0], 0))
+        first_terms = {1: float_tile(2 * V, "first_terms1", (3, 0, 0))}
+        modulate(first_terms[1][:], of_pair(gates[0], 1), of_pair(sampled[0], 1))
         for h in PAIRS:
             gate_pair(1, h)
         prepare(3, 1)
-        rest = V - SCALAR_SHARE_TAP1
-        late_part = float_tile(rest + V, "late_part", (3, 1, 0))
-        gather(late_part[:, :rest], rows[0, 0][:].indirect(pos_lists[1][:, SCALAR_SHARE_TAP1 // 16 :]), "vector")
-        gather(late_part[:, rest:], rows[0, 1][:].indirect(pos_lists[1][:]), "vector")
-        terms[1] = float_tile(PACK * V, "terms1", (3, 1, 2))
-        for t in (2, 3):
-            modulate_sets(1, (t,))
-        for part, columns in ((early_part, slice(0, SCALAR_SHARE_TAP1)), (late_part, slice(SCALAR_SHARE_TAP1, 2 * V))):
-            modulate(terms[1][:, columns], gates[1][:, columns], part[:])
-        partial = keep.tile([P, PACK * V], F32, name="partial")
-        on_gpsimd, on_vector = slice(0, GPSIMD_SHARE_SUM), slice(GPSIMD_SHARE_SUM, PACK * V)
-        nc.vector.tensor_tensor(partial[:, on_vector], terms[0][:, on_vector], terms[1][:, on_vector], ADD)
-        nc.gpsimd.tensor_tensor(partial[:, on_gpsimd], terms[0][:, on_gpsimd], terms[1][:, on_gpsimd], ADD)
-        sample(2, (2, 3), "vector", (3, 0, 0))
-        sample(2, (0, 1), "vector", (3, 0, 1))
+        first_terms[0] = float_tile(2 * V, "first_terms0", (3, 1, 0))
+        modulate(first_terms[0][:], of_pair(gates[0], 0), of_pair(sampled[0], 0))
+        second_terms = float_tile(PACK * V, "second_terms", (3, 1, 2))
+        for t in SETS:
+            modulate(of_set(second_terms, t), of_set(gates[1], t), sampled[1, (t,)][:])
+        partial = {3: float_tile(V, "partial3"), 2: float_tile(V, "partial2", (2, 1, 0))}
+        nc.vector.tensor_tensor(partial[3][:], of_set(first_terms[1], 1), of_set(second_terms, 3), ADD)
+        nc.gpsimd.tensor_tensor(partial[2][:], of_set(first_terms[1], 0), of_set(second_terms, 2), ADD)
+        partial_pair = float_tile(2 * V, "partial_pair")
+        nc.gpsimd.tensor_tensor(partial_pair[:], first_terms[0][:], of_pair(second_terms, 0), ADD)
+        for t in range(2):
+            partial[t] = of_set(partial_pair, t)
+        sample(2, (2, 3), "vector")
+        sample(2, (0, 1), "vector")
         for h in PAIRS:
             gate_pair(2, h)
         result = float_tile(PACK * V, "result")
@@ -275,7 +270,7 @@ def tile_picked_zmodd_tanh_po_kernel(
             modulate(last[t][:, columns], of_set(gates[2], t)[:, columns], of_set(sampled[2, sets], t % 2)[:, columns])
 
         def add_last(t, columns):
-            nc.vector.tensor_tensor(of_set(result, t)[:, columns], of_set(partial, t)[:, columns], last[t][:, columns], ADD)
+            nc.vector.tensor_tensor(of_set(result, t)[:, columns], partial[t][:, columns], last[t][:, columns], ADD)
 
         whole = slice(0, V)
         halves = [slice(a * HALF, (a + 1) * HALF) for a in range(2)]

@@ -32,6 +32,7 @@ SETS = (2, 3, 0, 1)
 UNIT_BYTES = PACK * N * 4
 PLACE_BYTES = UNIT_BYTES // 4
 HALF_LIST = S // 2
+GPSIMD_SHARE_SUM = 896
 SCALAR_SHARE_FIRST = 32
 SCALAR_SHARE_OUT = (48, 32)
 
@@ -238,53 +239,39 @@ def tile_picked_zmodd_tanh_po_kernel(
         prepare(2, 1)
         sample(1, (1,), "vector", (2, 1, 0))
         prepare(3, 0)
-        first_terms = {1: float_tile(2 * V, "first_terms1", (3, 0, 0))}
-        modulate(first_terms[1][:], of_pair(gates[0], 1), of_pair(sampled[0], 1))
         for h in PAIRS:
             gate_pair(1, h)
         prepare(3, 1)
-        first_terms[0] = float_tile(2 * V, "first_terms0", (3, 1, 0))
-        modulate(first_terms[0][:], of_pair(gates[0], 0), of_pair(sampled[0], 0))
-        second_terms = float_tile(PACK * V, "second_terms", (3, 1, 2))
+        terms = [float_tile(PACK * V, "terms%d" % d, (3, 1, 2 * d)) for d in range(2)]
+        modulate(terms[0][:], gates[0][:], sampled[0][:])
         for t in SETS:
-            modulate(of_set(second_terms, t), of_set(gates[1], t), sampled[1, (t,)][:])
-        partial = {3: float_tile(V, "partial3"), 2: float_tile(V, "partial2", (2, 1, 0))}
-        nc.vector.tensor_tensor(partial[3][:], of_set(first_terms[1], 1), of_set(second_terms, 3), ADD)
-        nc.gpsimd.tensor_tensor(partial[2][:], of_set(first_terms[1], 0), of_set(second_terms, 2), ADD)
-        partial_pair = float_tile(2 * V, "partial_pair")
-        nc.gpsimd.tensor_tensor(partial_pair[:], first_terms[0][:], of_pair(second_terms, 0), ADD)
-        for t in range(2):
-            partial[t] = of_set(partial_pair, t)
+            modulate(of_set(terms[1], t), of_set(gates[1], t), sampled[1, (t,)][:])
+        partial = keep.tile([P, PACK * V], F32, name="partial")
+        on_gpsimd, on_vector = slice(0, GPSIMD_SHARE_SUM), slice(GPSIMD_SHARE_SUM, PACK * V)
+        nc.vector.tensor_tensor(partial[:, on_vector], terms[0][:, on_vector], terms[1][:, on_vector], ADD)
+        nc.gpsimd.tensor_tensor(partial[:, on_gpsimd], terms[0][:, on_gpsimd], terms[1][:, on_gpsimd], ADD)
         sample(2, (2, 3), "vector")
         sample(2, (0, 1), "vector")
         for h in PAIRS:
             gate_pair(2, h)
         result = float_tile(PACK * V, "result")
         out_rows = out_0.rearrange("(p t) v -> p (t v)", t=PACK)
-        last = {}
-
-        def modulate_last(t, columns):
-            if t not in last:
-                last[t] = float_tile(V, "last%d" % t, tag="last%d" % (t % 2))
-            sets = (2 * (t // 2), 2 * (t // 2) + 1)
-            modulate(last[t][:, columns], of_set(gates[2], t)[:, columns], of_set(sampled[2, sets], t % 2)[:, columns])
-
-        def add_last(t, columns):
-            nc.vector.tensor_tensor(of_set(result, t)[:, columns], partial[t][:, columns], last[t][:, columns], ADD)
-
-        whole = slice(0, V)
         halves = [slice(a * HALF, (a + 1) * HALF) for a in range(2)]
+        last_terms = {t: float_tile(V, "last_terms%d" % t) for t in (2, 3)}
         for t in (2, 3):
-            modulate_last(t, whole)
+            modulate(last_terms[t][:], of_set(gates[2], t), of_set(sampled[2, (2, 3)], t - 2))
         for t in (2, 3):
-            add_last(t, whole)
+            nc.vector.tensor_tensor(of_set(result, t), of_set(partial, t), last_terms[t][:], ADD)
         nc.sync.dma_start(of_pair(out_rows, 1), of_pair(result, 1))
-        modulate_last(0, whole)
+        last_pair = float_tile(2 * V, "last_pair", tag="last_terms2")
+
+        def half_of_pair0(tile, columns):
+            return of_pair(tile, 0).rearrange("p (u v) -> p u v", u=2)[:, :, columns]
+
         for columns in halves:
-            modulate_last(1, columns)
-        add_last(0, whole)
+            modulate(half_of_pair0(last_pair, columns), half_of_pair0(gates[2], columns), half_of_pair0(sampled[2, (0, 1)], columns))
         for columns in halves:
-            add_last(1, columns)
+            nc.vector.tensor_tensor(half_of_pair0(result, columns), half_of_pair0(partial, columns), half_of_pair0(last_pair, columns), ADD)
         nc.sync.dma_start(of_pair(out_rows, 0), of_pair(result, 0))
 
         out_rounded = keep.tile([P, V * PACK], BF16, name="out_rounded", align_bytes=MX_ALIGN)

from contextlib import ExitStack

import concourse.mybir as mybir

K, T, S, V, N = 1024, 1024, 512, 256, 512
FLOPS = 2 * 4 * K * S * N

F32 = mybir.dt.float32
BF16 = mybir.dt.bfloat16
I32 = mybir.dt.int32
U32 = mybir.dt.uint32
U16 = mybir.dt.uint16
U8 = mybir.dt.uint8
FP8X4 = mybir.dt.float8_e4m3fn_x4
MULT = mybir.AluOpType.mult
ADD = mybir.AluOpType.add
SUBTRACT = mybir.AluOpType.subtract
SIGMOID = mybir.ActivationFunctionType.Sigmoid
COPY = mybir.ActivationFunctionType.Copy

P = 128
PACK = 4
PASSES = 2
QUADRANTS = 4
QUADRANT = 32
LIVE = 4
MX_ALIGN = 64
LINE = 4
HALF = V // 2
PAIRS = (1, 0)
SETS = (2, 3, 0, 1)
UNIT_BYTES = PACK * N * 4
PLACE_BYTES = UNIT_BYTES // 4
HALF_LIST = S // 2
GPSIMD_SHARE_SUM = 896
SCALAR_SHARE_FIRST = 32
SCALAR_SHARE_OUT = (48, 32)


def tile_picked_zmodd_tanh_po_kernel(
    tc, x_words, x_scales, w0, w1, w2, w3, offs, cen, pos1, pos2, pos3, out_0, out_1, out_2
):
    nc = tc.nc
    weights = [w0, w1, w2, w3]
    with ExitStack() as ctx:
        keep = ctx.enter_context(tc.tile_pool(name="keep", bufs=1))
        stage = ctx.enter_context(tc.tile_pool(name="stage", bufs=1))
        psum = ctx.enter_context(tc.psum_pool(name="psum", bufs=2))

        def float_tile(columns, name, after=None, tag=""):
            if after is None:
                return keep.tile([P, columns], F32, name=name, tag=tag, align_bytes=MX_ALIGN)
            w, g, place = after
            offset = (PASSES * w + g) * UNIT_BYTES + place * PLACE_BYTES
            return stage.tile([P, columns], F32, name=name, offset=offset, align_bytes=MX_ALIGN)

        def of_set(tile, t):
            return tile[:, t * V : (t + 1) * V]

        def of_pair(tile, h):
            return tile[:, 2 * h * V : 2 * (h + 1) * V]

        plane = keep.tile([P, T], U8, name="plane", align_bytes=MX_ALIGN)
        nc.vector.memset(plane[:].bitcast(I32), 0)
        zero = keep.tile([P, 1], F32, name="zero")
        nc.vector.memset(zero[:], 0.0)
        one_half = keep.tile([P, 1], F32, name="one_half")
        nc.scalar.activation(one_half[:], zero[:], SIGMOID)

        def load_list(name, dram):
            tile = keep.tile(list(dram.shape), U16, name=name)
            nc.sync.dma_start(tile[:], dram)
            return tile

        def load_words(g):
            tile = keep.tile([P, T], I32, name="words%d" % g)
            nc.sync.dma_start(tile[:], x_words[g].rearrange("p c r -> p (c r)").bitcast(I32))
            return tile

        raw = {}

        def load_weight(w, g):
            offset = (PASSES * w + g) * UNIT_BYTES
            raw[w, g] = stage.tile([P, PACK, N], F32, name="raw%d%d" % (w, g), offset=offset, align_bytes=MX_ALIGN)
            k_rows = weights[w][g * P * PACK : (g + 1) * P * PACK, :]
            nc.sync.dma_start(raw[w, g][:], k_rows.rearrange("(p j) m -> p j m", j=PACK))

        words = [load_words(0)]
        offs_list = load_list("offs_list", offs)
        for q in range(QUADRANTS):
            nc.sync.dma_start(
                plane[QUADRANT * q : QUADRANT * q + PASSES * LIVE, :].bitcast(I32),
                x_scales[:, LIVE * q : LIVE * (q + 1), :].bitcast(I32),
            )
        load_weight(0, 0)
        load_weight(0, 1)
        words.append(load_words(1))
        load_weight(1, 0)
        pos_lists = [load_list("pos1_list", pos1), load_list("pos2_list", pos2)]
        load_weight(1, 1)
        cen_list = load_list("cen_list", cen)
        for w in (2, 3):
            for g in range(PASSES):
                load_weight(w, g)
        pos_lists.append(load_list("pos3_list", pos3))

        picked = [keep.tile([P, S], U32, name="picked%d" % g, align_bytes=MX_ALIGN) for g in range(PASSES)]
        picked_scales = keep.tile([P, S], U8, name="picked_scales", align_bytes=MX_ALIGN)

        def pick_words(g, entries):
            offsets = offs_list[:, entries.start // 16 : entries.stop // 16]
            nc.vector.tensor_copy(picked[g][:, entries], words[g][:].bitcast(U32).indirect(offsets))

        list_halves = [slice(a * HALF_LIST, (a + 1) * HALF_LIST) for a in range(2)]
        pick_words(0, slice(0, S))
        nc.vector.tensor_copy(picked_scales[:], plane[:].indirect(offs_list[:]))

        rounded = {}
        banks = {}
        rows = {}
        gates = {}
        sampled = {}

        def rounded_tag(w, g, h):
            return "rounded%d%d%d" % (w, g, h)

        def round_pair(w, g, h, scalar_share):
            tag = rounded_tag(w, g, h)
            tile = keep.tile([P, 2, P, PACK], BF16, name=tag, tag=tag, align_bytes=MX_ALIGN)
            src = raw[w, g][:].rearrange("p j (i t) -> p i j t", t=PACK)[:, :, :, 2 * h : 2 * h + 2]
            dst = tile[:].rearrange("p u i j -> p i j u")
            if scalar_share > 0:
                nc.scalar.copy(dst[:, :scalar_share], src[:, :scalar_share])
            if scalar_share < P:
                nc.vector.tensor_copy(dst[:, scalar_share:], src[:, scalar_share:])
            rounded[w, g, h] = tile

        quantised = {}

        def quantise_pair(w, g, h):
            codes = keep.tile([P, 2 * P], U32, name="codes%d%d%d" % (w, g, h), align_bytes=MX_ALIGN)
            scales = keep.tile([P, 2 * P], U8, name="scales%d%d%d" % (w, g, h), align_bytes=MX_ALIGN)
            nc.vector.quantize_mx(
                out=codes[:].bitcast(FP8X4),
                scales=scales[:],
                in_=rounded[w, g, h][:].rearrange("p u i j -> p (u i j)"),
            )
            quantised[w, g, h] = (codes, scales)

        def multiply_pair(w, g, h, entries):
            codes, scales = quantised[w, g, h]
            for u in range(2):
                t = 2 * h + u
                if g == 0:
                    banks[w, t, entries.start] = psum.tile([P, S], F32, name="bank%d" % t)
                columns = slice(u * P, (u + 1) * P)
                nc.tensor.matmul_mx(
                    out=banks[w, t, entries.start][:, entries],
                    lhsT=codes[:, columns].bitcast(FP8X4),
                    lhsT_scale=scales[:, columns],
                    rhs=picked[g][:, entries].bitcast(FP8X4),
                    rhs_scale=picked_scales[LIVE * g :, entries],
                    start=(g == 0),
                    stop=(g == PASSES - 1),
                )

        def prepare(w, g):
            for h in PAIRS:
                round_pair(w, g, h, 0)
            for h in PAIRS:
                quantise_pair(w, g, h)
                multiply_pair(w, g, h, slice(0, S))

        def leave(w, t):
            rows[w, t] = float_tile(S, "rows%d%d" % (w, t))
            if (w, t) == (1, SETS[0]):
                nc.scalar.activation(rows[w, t][:], banks[w, t, 0][:], COPY, scale=4.0)
            else:
                nc.scalar.copy(rows[w, t][:], banks[w, t, 0][:])

        def gather(out, window, engine):
            if engine == "scalar":
                nc.scalar.activation(out, window, COPY)
            else:
                nc.vector.tensor_copy(out, window)

        def gate_pair(d, h):
            if d not in gates:
                gates[d] = float_tile(PACK * V, "gates%d" % d)
            for t in (2 * h, 2 * h + 1):
                leave(d + 1, t)
            for t in (2 * h, 2 * h + 1):
                width = HALF if (d, t) == (2, 1) else V
                scale = one_half[:] if (d, t) == (0, SETS[0]) else 2.0
                for first in range(0, V, width):
                    sums = rows[d + 1, t][:].indirect(cen_list[:, first // 16 : (first + width) // 16])
                    nc.scalar.activation(of_set(gates[d], t)[:, first : first + width], sums, SIGMOID, scale=scale)

        def sample(d, sets, engine, after=None):
            tile = float_tile(len(sets) * V, "sampled%d%d" % (d, sets[0]), after)
            sampled[d, sets] = tile
            for u, t in enumerate(sets):
                gather(of_set(tile, u), rows[0, t][:].indirect(pos_lists[d][:]), engine)

        def modulate(out, gate, sample):
            nc.vector.scalar_tensor_tensor(out, gate, 0.5, sample, SUBTRACT, MULT)

        first_pieces = {1: list_halves, 0: [slice(0, S)]}
        round_pair(0, 0, 1, 0)
        round_pair(0, 0, 0, P)
        for h in PAIRS:
            quantise_pair(0, 0, h)
            for entries in first_pieces[h]:
                multiply_pair(0, 0, h, entries)
        round_pair(0, 1, 1, SCALAR_SHARE_FIRST)
        round_pair(0, 1, 0, P)
        quantise_pair(0, 1, 1)
        for entries in list_halves:
            pick_words(1, entries)
        quantise_pair(0, 1, 0)
        for h in PAIRS:
            for t in (2 * h, 2 * h + 1):
                rows[0, t] = float_tile(S, "rows0%d" % t)
            for entries in first_pieces[h]:
                multiply_pair(0, 1, h, entries)
                for t in (2 * h, 2 * h + 1):
                    nc.scalar.activation(rows[0, t][:, entries], banks[0, t, entries.start][:, entries], COPY, scale=2.0)
        prepare(1, 0)
        sampled[0] = float_tile(PACK * V, "sampled0")
        for t in SETS:
            gather(of_set(sampled[0], t), rows[0, t][:].indirect(pos_lists[0][:]), "scalar")
        sample(1, (0,), "scalar")
        sample(1, (2,), "vector", (1, 0, 0))
        prepare(1, 1)
        prepare(2, 0)
        sample(1, (3,), "vector", (2, 0, 0))
        for h in PAIRS:
            gate_pair(0, h)
        prepare(2, 1)
        sample(1, (1,), "vector", (2, 1, 0))
        prepare(3, 0)
        for h in PAIRS:
            gate_pair(1, h)
        prepare(3, 1)
        terms = [float_tile(PACK * V, "terms%d" % d, (3, 1, 2 * d)) for d in range(2)]
        modulate(terms[0][:], gates[0][:], sampled[0][:])
        for t in SETS:
            modulate(of_set(terms[1], t), of_set(gates[1], t), sampled[1, (t,)][:])
        partial = keep.tile([P, PACK * V], F32, name="partial")
        on_gpsimd, on_vector = slice(0, GPSIMD_SHARE_SUM), slice(GPSIMD_SHARE_SUM, PACK * V)
        nc.vector.tensor_tensor(partial[:, on_vector], terms[0][:, on_vector], terms[1][:, on_vector], ADD)
        nc.gpsimd.tensor_tensor(partial[:, on_gpsimd], terms[0][:, on_gpsimd], terms[1][:, on_gpsimd], ADD)
        sample(2, (2, 3), "vector")
        sample(2, (0, 1), "vector")
        for h in PAIRS:
            gate_pair(2, h)
        result = float_tile(PACK * V, "result")
        out_rows = out_0.rearrange("(p t) v -> p (t v)", t=PACK)
        halves = [slice(a * HALF, (a + 1) * HALF) for a in range(2)]
        last_terms = {t: float_tile(V, "last_terms%d" % t) for t in (2, 3)}
        for t in (2, 3):
            modulate(last_terms[t][:], of_set(gates[2], t), of_set(sampled[2, (2, 3)], t - 2))
        for t in (2, 3):
            nc.vector.tensor_tensor(of_set(result, t), of_set(partial, t), last_terms[t][:], ADD)
        nc.sync.dma_start(of_pair(out_rows, 1), of_pair(result, 1))
        last_pair = float_tile(2 * V, "last_pair", tag="last_terms2")

        def half_of_pair0(tile, columns):
            return of_pair(tile, 0).rearrange("p (u v) -> p u v", u=2)[:, :, columns]

        for columns in halves:
            modulate(half_of_pair0(last_pair, columns), half_of_pair0(gates[2], columns), half_of_pair0(sampled[2, (0, 1)], columns))
        for columns in halves:
            nc.vector.tensor_tensor(half_of_pair0(result, columns), half_of_pair0(partial, columns), half_of_pair0(last_pair, columns), ADD)
        nc.sync.dma_start(of_pair(out_rows, 0), of_pair(result, 0))

        out_rounded = keep.tile([P, V * PACK], BF16, name="out_rounded", align_bytes=MX_ALIGN)
        out_codes = keep.tile([P, V], I32, name="out_codes", align_bytes=MX_ALIGN)
        out_scales = keep.tile([P, V], U8, name="out_scales", align_bytes=MX_ALIGN)
        dst = out_rounded[:].rearrange("p (c i t) -> p c t i", i=LINE, t=PACK)
        src = result[:].rearrange("p (t c i) -> p c t i", i=LINE, t=PACK)
        for a in range(2):
            first, last = a * HALF // LINE, (a + 1) * HALF // LINE
            cut = first + SCALAR_SHARE_OUT[a] // LINE
            nc.scalar.copy(dst[:, first:cut], src[:, first:cut])
            nc.vector.tensor_copy(dst[:, cut:last], src[:, cut:last])
        for a in range(2):
            columns = slice(a * HALF, (a + 1) * HALF)
            nc.vector.quantize_mx(
                out=out_codes[:, columns].bitcast(FP8X4),
                scales=out_scales[:, columns],
                in_=out_rounded[:, PACK * columns.start : PACK * columns.stop],
            )
        nc.sync.dma_start(out_1[0].rearrange("p c r -> p (c r)").bitcast(I32), out_codes[:])
        for q in range(QUADRANTS):
            queue = nc.scalar if q % 2 == 0 else nc.sync
            queue.dma_start(
                out_2[0, LIVE * q : LIVE * (q + 1), :].bitcast(I32),
                out_scales[QUADRANT * q : QUADRANT * q + LIVE, :].bitcast(I32),
            )
